import numpy as np
import ml_dtypes


def mxq(x, axis, fmt="e4m3"):
    dtype, down = {"e4m3": (ml_dtypes.float8_e4m3fn, 7), "e5m2": (ml_dtypes.float8_e5m2, 14)}[fmt]
    v = np.moveaxis(np.asarray(x, np.float32).astype(ml_dtypes.bfloat16).astype(np.float64), axis, -1)
    blocks = v.reshape(v.shape[:-1] + (-1, 32))
    amax = np.abs(blocks).max(-1, keepdims=True)
    byte = np.maximum(np.where(amax > 0, np.frexp(amax)[1] - 1 + 127, 0) - down, 1)
    scale = np.exp2(byte - 127.0)
    codes = (blocks / scale).astype(np.float32).astype(dtype).astype(np.float64)
    return np.moveaxis((codes * scale).reshape(v.shape), -1, axis)


WIDE = False


def mx_kscale(k):
    if not WIDE:
        return np.ones(k)
    levels = np.array([10, -10, 5, -5, 0])
    if k % 512:
        return np.exp2(np.random.permutation(np.resize(levels, k // 32))).repeat(32)
    a = np.empty((k // 512, 16))
    for p in range(k // 512):
        a[p, :8] = np.random.permutation(np.resize(levels, 8))
        for g in range(8):
            far = levels[np.abs(levels - a[p, g]) >= 10]
            a[p, g + 8] = far[np.random.randint(len(far))]
    return np.exp2(a.ravel()).repeat(32)


def f64(x):
    return np.asarray(x).astype(np.float64)


def striped(idx):
    return np.tile(idx.reshape(-1, 16).T, (8, 1)).astype(np.uint16)


def unstriped(offs):
    return offs[:16].T.reshape(-1).astype(np.int64)


def striped8(idx):
    return np.concatenate([x.reshape(-1, 16).T for x in idx]).astype(np.uint16)


def runs(offs, k):
    lists = np.stack([offs[16 * r : 16 * r + 16].T.reshape(-1) for r in range(8)]).astype(np.int64)
    return lists[np.arange(k) % 512 // 64]


def pack_weight(w):
    k, n = w.shape
    w = f64(np.asarray(w, np.float32).astype(ml_dtypes.bfloat16)).reshape(k // 32, 32, n)
    amax = np.abs(w).max(1)
    byte = np.clip(np.where(amax > 0, np.frexp(amax)[1] - 1 + 127 - 7, 1), 1, 254)
    scaled = (w * np.exp2(127.0 - byte)[:, None, :]).reshape(k, n).astype(np.float32)
    words = np.ascontiguousarray(scaled.reshape(k // 512, 128, 4, n).transpose(0, 1, 3, 2)).astype(ml_dtypes.float8_e4m3fn).view(np.uint8)
    return words, np.ascontiguousarray(byte.astype(np.uint8).reshape(k // 512, 16, n))


def unpack_weight(words, scales):
    g, p, n, _ = words.shape
    vals = np.ascontiguousarray(words).view(ml_dtypes.float8_e4m3fn).astype(np.float64) * np.repeat(np.exp2(scales.astype(np.float64) - 127.0), 8, axis=1)[..., None]
    return vals.transpose(0, 1, 3, 2).reshape(g * 512, n)


E2M1 = np.array([0.0, 0.5, 1.0, 1.5, 2.0, 3.0, 4.0, 6.0, -0.0, -0.5, -1.0, -1.5, -2.0, -3.0, -4.0, -6.0])


def pack_fp4(w):
    k, n = w.shape
    w = f64(np.asarray(w, np.float32).astype(ml_dtypes.bfloat16)).reshape(k // 32, 32, n)
    amax = np.abs(w).max(1)
    mant, ex = np.frexp(amax / 6.0)
    byte = np.clip(np.where(amax > 0, np.where(mant > 0.5, ex, ex - 1) + 127, 1), 1, 254)
    scaled = (w * np.exp2(127.0 - byte)[:, None, :]).reshape(k, n).astype(np.float32)
    c = np.ascontiguousarray(scaled.reshape(k // 512, 128, 4, n).transpose(0, 1, 3, 2)).astype(ml_dtypes.float4_e2m1fn).view(np.uint8) & 0xF
    words = (c[..., 0::2] | (c[..., 1::2] << 4)).reshape(k // 512, 128, 2 * n)
    return np.ascontiguousarray(words), np.ascontiguousarray(byte.astype(np.uint8).reshape(k // 512, 16, n))


def unpack_fp4(words, scales):
    g, _, n = scales.shape
    words = np.ascontiguousarray(words).reshape(g, 128, n, 2)
    nib = np.empty((g, 128, n, 4), np.uint8)
    nib[..., 0::2] = words & 0xF
    nib[..., 1::2] = words >> 4
    vals = E2M1[nib] * np.repeat(np.exp2(scales.astype(np.float64) - 127.0), 8, axis=1)[..., None]
    return vals.transpose(0, 1, 3, 2).reshape(g * 512, n)


def sigmoid(v):
    return 1.0 / (1.0 + np.exp(-np.maximum(v, -700.0)))

def planes(y):
    n, m = y.shape
    v = y.astype(np.float32).astype(ml_dtypes.bfloat16).astype(np.float64).reshape(n // 32, 32, m)
    top = np.abs(v).max(1)
    byte = np.clip(np.where(top > 0, np.frexp(top)[1] - 1 + 127 - 7, 1), 1, 254)
    codes = (v * np.exp2(127.0 - byte)[:, None, :]).reshape(n, m).astype(np.float32).astype(ml_dtypes.float8_e4m3fn).view(np.uint8)
    words = codes.reshape(n // 512, 128, 4, m).transpose(0, 1, 3, 2)
    return np.ascontiguousarray(words), np.ascontiguousarray(byte.astype(np.uint8).reshape(n // 512, 16, m))


K, T, S, V, N, H = 512, 2048, 512, 512, 512, 512


def setup_inputs():
    n = np.random.standard_normal
    s = mx_kscale(K)[:, None]
    u = mx_kscale(S)
    packed_xT = pack_weight(n((K, T)) * s)
    packed_w1 = pack_fp4(n((K, H)) / np.sqrt(K) / s)
    packed_w2 = pack_fp4(n((K, H)) / np.sqrt(K) / s)
    return {
        "x_words": packed_xT[0],
        "x_scales": packed_xT[1],
        "w1_words": packed_w1[0],
        "w1_scales": packed_w1[1],
        "w2_words": packed_w2[0],
        "w2_scales": packed_w2[1],
        "gk": (np.random.uniform(0.5, 1.5, (H, 1)) * u[:, None]).astype(np.float32),
        "gq": (np.random.uniform(0.5, 1.5, (H, 1)) / u[:, None]).astype(np.float32),
        "wv": (n((K, N)) / np.sqrt(K) / s).astype(np.float32),
        "gi": (np.random.uniform(0.5, 1.5, (S, 1)) / u[:, None]).astype(np.float32),
        "res": n((N, V)).astype(np.float32),
        "gt": (np.random.uniform(0.5, 1.5, (S, 1)) * u[:, None]).astype(np.float32),
        "offs": striped(np.random.permutation(T)[:S]),
        "qs": striped(np.random.permutation(T)[:V]),
        "nb": striped8(np.stack([np.random.permutation(V) for _ in range(8)])),
    }


def reference(x_words, x_scales, w1_words, w1_scales, w2_words, w2_scales, gk, gq, wv, gi, res, gt, offs, qs, nb):
    xq = unpack_weight(x_words, x_scales)[:, unstriped(offs)]
    val = xq.T @ mxq(f64(wv), 0, "e4m3")
    zv = f64(gi) * val
    kf = unpack_fp4(w1_words, w1_scales).T @ xq
    z = f64(gk) * kf
    x_qs = unpack_weight(x_words, x_scales)[:, unstriped(qs)]
    qf = unpack_fp4(w2_words, w2_scales).T @ x_qs
    z2 = f64(gq) * qf
    s = 0.0625 * ((mxq(z, 0, "e4m3").T @ mxq(z2, 0, "e4m3")))
    zp = f64(gt) * (sigmoid(s + s[np.arange(S)[:, None], runs(nb, S)]))
    out_0 = f64(res) + 0.0625 * ((mxq(zv, 0, "e4m3").T @ mxq(zp, 0, "e4m3")))
    return (out_0,) + planes(out_0)

@@ -1,0 +1,276 @@
+from contextlib import ExitStack
+
+import concourse.mybir as mybir
+from concourse.masks import make_identity
+
+K, T, S, V, N, H = 512, 2048, 512, 512, 512, 512
+FLOPS = 5 * 2 * 512 * 512 * 512
+
+F32 = mybir.dt.float32
+BF16 = mybir.dt.bfloat16
+I32 = mybir.dt.int32
+U32 = mybir.dt.uint32
+U16 = mybir.dt.uint16
+U8 = mybir.dt.uint8
+FP8X4 = mybir.dt.float8_e4m3fn_x4
+FP4X4 = mybir.dt.float4_e2m1fn_x4
+ACT = mybir.ActivationFunctionType
+ALU = mybir.AluOpType
+
+P = 128
+W = 512
+HALF = 256
+SIXTEENTH = 0.0625
+
+
+def tile_picked_listsmooth_sigmoid_po_kernel(
+    tc, x_words, x_scales, w1_words, w1_scales, w2_words, w2_scales, gk, gq, wv, gi, res, gt, offs, qs, nb, out_0, out_1, out_2
+):
+    nc = tc.nc
+    with ExitStack() as ctx:
+        lists = ctx.enter_context(tc.tile_pool(name="lists", bufs=1))
+        sb = ctx.enter_context(tc.tile_pool(name="sb", bufs=1))
+        psum = ctx.enter_context(tc.psum_pool(name="psum", bufs=8))
+
+        def new(name, shape, dtype):
+            return sb.tile(shape, dtype, name=name, align_bytes=64)
+
+        def bank(name):
+            return psum.tile([P, W], F32, name=name, tag="bank")
+
+        qs_sb = lists.tile([P, W // 16], U16, name="qs_sb")
+        offs_sb = lists.tile([P, W // 16], U16, name="offs_sb")
+        nb_sb = lists.tile([P, W // 16], U16, name="nb_sb")
+        xs = new("xs", [P, T], U8)
+        xw = sb.tile([P, T], I32, name="xw", tag="xw_then_res", align_bytes=64)
+        nc.vector.memset(xs[:].bitcast(I32), 0)
+        w_raw_s = [new("w%d_raw_s" % j, [P, W], U8) for j in (2, 1)]
+        for raw_s in w_raw_s:
+            nc.vector.memset(raw_s[:].bitcast(I32), 0)
+        g_rows = new("g_rows", [P, P], F32)
+        nc.vector.memset(g_rows[:], 0.0)
+        ident = new("ident", [P, P], F32)
+        make_identity(nc, ident[:])
+        warm = new("warm", [P, 1], F32)
+        nc.scalar.activation(warm[:], ident[:, 0:1], ACT.Sigmoid)
+
+        nc.sync.dma_start(qs_sb[:], qs)
+        nc.sync.dma_start(offs_sb[:], offs)
+        for q in range(4):
+            nc.sync.dma_start(xs[32 * q : 32 * q + 4, :].bitcast(I32), x_scales[0, 4 * q : 4 * q + 4, :].bitcast(I32))
+
+        def load_words(name, words):
+            raw_w = new(name + "_raw_w", [P, 2 * W], U8)
+            nc.sync.dma_start(raw_w[:].bitcast(I32), words[0].bitcast(I32))
+            return raw_w
+
+        def load_scales(scales, raw_s):
+            for q in range(4):
+                nc.sync.dma_start(raw_s[32 * q : 32 * q + 4, :].bitcast(I32), scales[0, 4 * q : 4 * q + 4, :].bitcast(I32))
+            return raw_s
+
+        def load_factor(engine, j, g):
+            engine.dma_start(
+                g_rows[4 * j : 4 * j + 4, :].rearrange("t (b r) -> t b r", r=8),
+                g.rearrange("(b t r) o -> t b (r o)", t=4, r=8),
+            )
+
+        w2_raw_w = load_words("w2", w2_words)
+        nc.sync.dma_start(xw[:], x_words[0].rearrange("p n t -> p (n t)").bitcast(I32))
+        w2_raw = (w2_raw_w, load_scales(w2_scales, w_raw_s[0]))
+        load_factor(nc.sync, 0, gq)
+        load_factor(nc.sync, 1, gk)
+        load_factor(nc.gpsimd, 2, gi)
+        load_factor(nc.gpsimd, 3, gt)
+        g_ps = bank("g_ps")
+        nc.tensor.transpose(g_ps[:, 0:P], g_rows[:], ident[:])
+        g_cols = new("g_cols", [P, 16], F32)
+        nc.scalar.copy(g_cols[:], g_ps[:, 0:16])
+        gq_c, gk_c, gi_c, gt_c = [g_cols[:, 4 * j : 4 * j + 4] for j in range(4)]
+        w1_raw = (load_words("w1", w1_words), load_scales(w1_scales, w_raw_s[1]))
+        wv_raw = new("wv_raw", [P, 4, W], F32)
+        nc.sync.dma_start(wv_raw[:], wv.rearrange("(p j) c -> p j c", j=4))
+        nc.sync.dma_start(nb_sb[:], nb)
+
+        def deal(engine, name, raw, width):
+            dealt = new(name, [P, width], U8)
+            engine.tensor_copy(
+                dealt[:].bitcast(I32).rearrange("p (t b u) -> p t b u", t=4, b=16),
+                raw[:].bitcast(I32).rearrange("p (b t u) -> p t b u", t=4, b=16),
+            )
+            return dealt
+
+        q_scale = new("q_scale", [P, W], U8)
+        nc.vector.tensor_copy(q_scale[:], xs[:].indirect(qs_sb[:]))
+        k_scale_raw = new("k_scale_raw", [P, W], U8)
+        nc.vector.tensor_copy(k_scale_raw[:], xs[:].indirect(offs_sb[:]))
+        k_scale = deal(nc.vector, "k_scale", k_scale_raw, W)
+        w2_w = deal(nc.gpsimd, "w2_w", w2_raw[0], 2 * W)
+        w2_s = deal(nc.gpsimd, "w2_s", w2_raw[1], W)
+        q_words = []
+        for h in range(2):
+            t_ = new("q_words%d" % h, [P, HALF], U32)
+            nc.vector.tensor_copy(t_[:], xw[:].bitcast(U32).indirect(qs_sb[:, 16 * h : 16 * h + 16]))
+            q_words.append(t_)
+        k_words = new("k_words", [P, W], U32)
+        nc.vector.tensor_copy(
+            k_words[:].rearrange("p (t b r) -> p b t r", t=4, b=16), xw[:].bitcast(U32).indirect(offs_sb[:])
+        )
+        w1_w = deal(nc.gpsimd, "w1_w", w1_raw[0], 2 * W)
+        w1_s = deal(nc.gpsimd, "w1_s", w1_raw[1], W)
+
+        res_sb = sb.tile([P, 4, W], F32, name="res_sb", tag="xw_then_res", align_bytes=64)
+        nc.sync.dma_start(res_sb[:], res.rearrange("(p t) v -> p t v", t=4))
+
+        def mx(out, lhs, lhs_s, rhs, rhs_s):
+            nc.tensor.matmul_mx(out=out, lhsT=lhs, lhsT_scale=lhs_s, rhs=rhs, rhs_scale=rhs_s, start=True, stop=True)
+
+        def fp4_slot(words, t):
+            return words[:, 2 * P * t : 2 * P * (t + 1)].bitcast(FP4X4)
+
+        def cols(c0, n):
+            return slice(c0, c0 + n)
+
+        def weave(engine_copy, woven, planes):
+            engine_copy(
+                woven.rearrange("p (c i t) -> p c t i", i=4, t=4), planes[:].rearrange("p t (c i) -> p c t i", i=4)
+            )
+            return woven
+
+        def quantise(codes, scales, woven):
+            nc.vector.quantize_mx(out=codes.bitcast(FP8X4), scales=scales, in_=woven)
+
+        def scaled_planes(name, lhs_slot, rhs, rhs_s, n, g):
+            planes = new(name + "_planes", [P, 4, n], BF16)
+            per_bank = W // n
+            for t0 in range(0, 4, per_bank):
+                acc = bank(name + "_acc%d" % t0)
+                for t in range(t0, t0 + per_bank):
+                    mx(acc[:, cols((t - t0) * n, n)], *lhs_slot(t), rhs, rhs_s)
+                for t in range(t0, t0 + per_bank):
+                    nc.scalar.activation(planes[:, t, :], acc[:, cols((t - t0) * n, n)], ACT.Copy, scale=g[:, t : t + 1])
+            return planes
+
+        def by_vector(name, woven, lhs_slot, rhs, rhs_s, g):
+            acc = bank(name + "_acc")
+            for t in range(4):
+                mx(acc[:, cols(t * P, P)], *lhs_slot(t), rhs, rhs_s)
+            nc.vector.tensor_tensor(
+                woven.rearrange("p (n t) -> p n t", t=4),
+                acc[:].rearrange("p (t n) -> p n t", t=4),
+                g.unsqueeze(1).to_broadcast([P, P, 4]),
+                ALU.mult,
+            )
+            return woven
+
+        def w2_slot(t):
+            return fp4_slot(w2_w, t), w2_s[:, cols(t * P, P)]
+
+        def w1_slot(t):
+            return fp4_slot(w1_w, t), w1_s[:, cols(t * P, P)]
+
+        def k_slot(t):
+            return k_words[:, cols(t * P, P)].bitcast(FP8X4), k_scale[:, cols(t * P, P)]
+
+        z2_c = new("z2_c", [P, W], U32)
+        z2_s = new("z2_s", [P, W], U8)
+        z_c = new("z_c", [P, W], U32)
+        z_s = new("z_s", [P, W], U8)
+        z2_woven = new("z2_woven", [P, 4 * W], BF16)
+        planes = scaled_planes("z2_0", w2_slot, q_words[0][:].bitcast(FP8X4), q_scale[:, 0:HALF], HALF, gq_c)
+        for c in (2, 3):
+            by_vector("z2_%d" % c, z2_woven[:, cols(4 * P * c, 4 * P)], w2_slot, q_words[1][:, cols((c - 2) * P, P)].bitcast(FP8X4), q_scale[:, cols(c * P, P)], gq_c)
+        weave(nc.vector.tensor_copy, z2_woven[:, 0 : 4 * HALF], planes)
+        z_woven0 = new("z_woven0", [P, 4 * P], BF16)
+        by_vector("z_0", z_woven0[:], w1_slot, k_words[:, 0:P].bitcast(FP8X4), k_scale[:, 0:P], gk_c)
+        quantise(z2_c[:], z2_s[:], z2_woven[:])
+        quantise(z_c[:, 0:P], z_s[:, 0:P], z_woven0[:])
+        rest = []
+        for c0, n in ((P, P), (HALF, HALF)):
+            planes = scaled_planes("z_%d" % c0, w1_slot, k_words[:, cols(c0, n)].bitcast(FP8X4), k_scale[:, cols(c0, n)], n, gk_c)
+            woven = new("z_woven%d" % c0, [P, 4 * n], BF16)
+            rest.append((c0, n, weave(nc.vector.tensor_copy, woven[:], planes)))
+        for c0, n, woven in rest:
+            quantise(z_c[:, cols(c0, n)], z_s[:, cols(c0, n)], woven)
+
+        windows, plains = [], []
+        for t in range(4):
+            acc = bank("s_acc%d" % t)
+            mx(acc[:], z_c[:, cols(t * P, P)].bitcast(FP8X4), z_s[:, cols(t * P, P)], z2_c[:].bitcast(FP8X4), z2_s[:])
+            window = sb.tile([P, W], F32, name="s_window%d" % t, tag="s_window%d" % t, align_bytes=64)
+            plain = new("s_plain%d" % t, [P, W], F32)
+            nc.scalar.activation(window[:], acc[:], ACT.Copy, scale=SIXTEENTH)
+            nc.sync.dma_start(plain[:], window[:])
+            windows.append(window)
+            plains.append(plain)
+
+        wv_woven = new("wv_woven", [P, 4 * W], BF16)
+        for h, copy in enumerate((nc.scalar.copy, nc.vector.tensor_copy)):
+            copy(
+                wv_woven[:].rearrange("p (t m j) -> p m j t", t=4, j=4)[:, 64 * h : 64 * h + 64],
+                wv_raw[:].rearrange("p j (m t) -> p m j t", t=4)[:, 64 * h : 64 * h + 64],
+            )
+        wv_c = new("wv_c", [P, W], U32)
+        wv_s = new("wv_s", [P, W], U8)
+        quantise(wv_c[:], wv_s[:], wv_woven[:])
+        zv_c = new("zv_c", [P, W], U32)
+        zv_s = new("zv_s", [P, W], U8)
+        zv_planes = scaled_planes("zv", k_slot, wv_c[:].bitcast(FP8X4), wv_s[:], W, gi_c)
+
+        zp_planes = []
+        for h in range(2):
+            sums = new("sums%d" % h, [P, 4, HALF], F32)
+            for t in range(4):
+                nc.vector.tensor_tensor(
+                    sums[:, t, :],
+                    windows[t][:].indirect(nb_sb[:, 16 * h : 16 * h + 16]),
+                    plains[t][:, cols(h * HALF, HALF)],
+                    ALU.add,
+                )
+            sig = new("sig%d" % h, [P, 4, HALF], F32)
+            nc.scalar.activation(sig[:], sums[:], ACT.Sigmoid)
+            planes = new("zp_planes%d" % h, [P, 4, HALF], BF16)
+            for t in range(4):
+                nc.scalar.activation(planes[:, t, :], sig[:, t, :], ACT.Copy, scale=gt_c[:, t : t + 1])
+            zp_planes.append(planes)
+
+        zv_woven = sb.tile([P, 4 * W], BF16, name="zv_woven", tag="s_window3", align_bytes=64)
+        quantise(zv_c[:], zv_s[:], weave(nc.vector.tensor_copy, zv_woven[:], zv_planes))
+
+        y_s = new("y_s", [P, W], U8)
+        out_rows = out_0.rearrange("(p t) v -> p t v", t=4)
+        out_words = out_1[0].rearrange("p n t -> p (n t)").bitcast(I32)
+        zp = []
+        for h in range(2):
+            woven = new("zp_woven%d" % h, [P, 4 * HALF], BF16)
+            woven = weave(nc.vector.tensor_copy, woven[:], zp_planes[h])
+            zp_c = new("zp_c%d" % h, [P, HALF], U32)
+            zp_s = new("zp_s%d" % h, [P, HALF], U8)
+            quantise(zp_c[:], zp_s[:], woven)
+            zp.append((zp_c, zp_s))
+        y_woven = []
+        for c in range(4):
+            zp_c, zp_s = zp[c // 2]
+            part = cols((c % 2) * P, P)
+            acc = bank("out_acc%d" % c)
+            for t in range(4):
+                mx(
+                    acc[:, cols(t * P, P)],
+                    zv_c[:, cols(t * P, P)].bitcast(FP8X4),
+                    zv_s[:, cols(t * P, P)],
+                    zp_c[:, part].bitcast(FP8X4),
+                    zp_s[:, part],
+                )
+            y = new("y%d" % c, [P, 4, P], F32)
+            nc.vector.scalar_tensor_tensor(
+                y[:], acc[:].rearrange("p (t n) -> p t n", t=4), SIXTEENTH, res_sb[:, :, cols(c * P, P)], ALU.mult, ALU.add
+            )
+            nc.sync.dma_start(out_rows[:, :, cols(c * P, P)], y[:])
+            woven = new("y_woven%d" % c, [P, 4 * P], BF16)
+            y_woven.append(weave(nc.vector.tensor_copy if c == 3 else nc.scalar.copy, woven[:], y))
+        for c in range(4):
+            y_c = new("y_c%d" % c, [P, P], U32)
+            quantise(y_c[:], y_s[:, cols(c * P, P)], y_woven[c])
+            nc.sync.dma_start(out_words[:, cols(c * P, P)], y_c[:].bitcast(I32))
+        for q in range(4):
+            (nc.scalar if q % 2 else nc.sync).dma_start(out_2[0, 4 * q : 4 * q + 4, :].bitcast(I32), y_s[32 * q : 32 * q + 4, :].bitcast(I32))

@@ -43,16 +43,16 @@ def tile_picked_listsmooth_sigmoid_po_kernel(
         nb_sb = lists.tile([P, W // 16], U16, name="nb_sb")
         xs = new("xs", [P, T], U8)
         xw = sb.tile([P, T], I32, name="xw", tag="xw_then_res", align_bytes=64)
-        nc.vector.memset(xs[:].bitcast(I32), 0)
+        nc.gpsimd.memset(xs[:].bitcast(I32), 0)
         w_raw_s = [new("w%d_raw_s" % j, [P, W], U8) for j in (2, 1)]
         for raw_s in w_raw_s:
             nc.vector.memset(raw_s[:].bitcast(I32), 0)
         g_rows = new("g_rows", [P, P], F32)
-        nc.vector.memset(g_rows[:], 0.0)
-        ident = new("ident", [P, P], F32)
-        make_identity(nc, ident[:])
+        nc.gpsimd.memset(g_rows[:], 0.0)
+        warm_in = new("warm_in", [P, 1], F32)
+        nc.vector.memset(warm_in[:], 0.0)
         warm = new("warm", [P, 1], F32)
-        nc.scalar.activation(warm[:], ident[:, 0:1], ACT.Sigmoid)
+        nc.scalar.activation(warm[:], warm_in[:], ACT.Sigmoid)
 
         nc.sync.dma_start(qs_sb[:], qs)
         nc.sync.dma_start(offs_sb[:], offs)
@@ -82,14 +82,18 @@ def tile_picked_listsmooth_sigmoid_po_kernel(
         load_factor(nc.sync, 1, gk)
         load_factor(nc.gpsimd, 2, gi)
         load_factor(nc.gpsimd, 3, gt)
+        ident = new("ident", [P, P], F32)
+        make_identity(nc, ident[:])
         g_ps = bank("g_ps")
         nc.tensor.transpose(g_ps[:, 0:P], g_rows[:], ident[:])
         g_cols = new("g_cols", [P, 16], F32)
         nc.scalar.copy(g_cols[:], g_ps[:, 0:16])
         gq_c, gk_c, gi_c, gt_c = [g_cols[:, 4 * j : 4 * j + 4] for j in range(4)]
+        wv_rows = wv.rearrange("(p j) c -> p j c", j=4)
+        wv_raw = [sb.tile([P, 4, HALF], F32, name="wv_raw%d" % h, tag="wv_raw%d" % h, align_bytes=64) for h in range(2)]
+        for h in range(2):
+            nc.sync.dma_start(wv_raw[h][:], wv_rows[:, :, h * HALF : (h + 1) * HALF])
         w1_raw = (load_words("w1", w1_words), load_scales(w1_scales, w_raw_s[1]))
-        wv_raw = new("wv_raw", [P, 4, W], F32)
-        nc.sync.dma_start(wv_raw[:], wv.rearrange("(p j) c -> p j c", j=4))
         nc.sync.dma_start(nb_sb[:], nb)
 
         def deal(engine, name, raw, width):
@@ -176,11 +180,14 @@ def tile_picked_listsmooth_sigmoid_po_kernel(
         z2_s = new("z2_s", [P, W], U8)
         z_c = new("z_c", [P, W], U32)
         z_s = new("z_s", [P, W], U8)
-        z2_woven = new("z2_woven", [P, 4 * W], BF16)
+        wv_woven = new("wv_woven", [P, 4 * W], BF16)
+        weave(nc.vector.tensor_copy, wv_woven[:, 0 : 4 * HALF], wv_raw[0])
+        z2_woven = sb.tile([P, 4 * W], BF16, name="z2_woven", tag="wv_raw0", align_bytes=64)
         planes = scaled_planes("z2_0", w2_slot, q_words[0][:].bitcast(FP8X4), q_scale[:, 0:HALF], HALF, gq_c)
         for c in (2, 3):
             by_vector("z2_%d" % c, z2_woven[:, cols(4 * P * c, 4 * P)], w2_slot, q_words[1][:, cols((c - 2) * P, P)].bitcast(FP8X4), q_scale[:, cols(c * P, P)], gq_c)
         weave(nc.vector.tensor_copy, z2_woven[:, 0 : 4 * HALF], planes)
+        weave(nc.scalar.copy, wv_woven[:, 4 * HALF :], wv_raw[1])
         z_woven0 = new("z_woven0", [P, 4 * P], BF16)
         by_vector("z_0", z_woven0[:], w1_slot, k_words[:, 0:P].bitcast(FP8X4), k_scale[:, 0:P], gk_c)
         quantise(z2_c[:], z2_s[:], z2_woven[:])
@@ -198,24 +205,30 @@ def tile_picked_listsmooth_sigmoid_po_kernel(
             acc = bank("s_acc%d" % t)
             mx(acc[:], z_c[:, cols(t * P, P)].bitcast(FP8X4), z_s[:, cols(t * P, P)], z2_c[:].bitcast(FP8X4), z2_s[:])
             window = sb.tile([P, W], F32, name="s_window%d" % t, tag="s_window%d" % t, align_bytes=64)
-            plain = new("s_plain%d" % t, [P, W], F32)
+            plain = [new("s_plain%d_%d" % (t, h), [P, HALF], F32) for h in range(2)]
             nc.scalar.activation(window[:], acc[:], ACT.Copy, scale=SIXTEENTH)
-            nc.sync.dma_start(plain[:], window[:])
+            nc.scalar.activation(plain[0][:], acc[:, 0:HALF], ACT.Copy, scale=SIXTEENTH)
+            nc.sync.dma_start(plain[1][:], window[:, HALF:])
             windows.append(window)
             plains.append(plain)
 
-        wv_woven = new("wv_woven", [P, 4 * W], BF16)
-        for h, copy in enumerate((nc.scalar.copy, nc.vector.tensor_copy)):
-            copy(
-                wv_woven[:].rearrange("p (t m j) -> p m j t", t=4, j=4)[:, 64 * h : 64 * h + 64],
-                wv_raw[:].rearrange("p j (m t) -> p m j t", t=4)[:, 64 * h : 64 * h + 64],
-            )
         wv_c = new("wv_c", [P, W], U32)
         wv_s = new("wv_s", [P, W], U8)
         quantise(wv_c[:], wv_s[:], wv_woven[:])
         zv_c = new("zv_c", [P, W], U32)
         zv_s = new("zv_s", [P, W], U8)
-        zv_planes = scaled_planes("zv", k_slot, wv_c[:].bitcast(FP8X4), wv_s[:], W, gi_c)
+        zv_planes = new("zv_planes", [P, 4, HALF], BF16)
+        for t0 in (0, 2):
+            acc = bank("zv_acc%d" % t0)
+            for t in (t0, t0 + 1):
+                mx(acc[:, cols((t - t0) * HALF, HALF)], *k_slot(t), wv_c[:, 0:HALF].bitcast(FP8X4), wv_s[:, 0:HALF])
+            for t in (t0, t0 + 1):
+                nc.scalar.activation(
+                    zv_planes[:, t, :].rearrange("p (u m) -> p u m", u=4),
+                    acc[:, cols((t - t0) * HALF, HALF)].rearrange("p (m u) -> p u m", u=4),
+                    ACT.Copy,
+                    scale=gi_c[:, t : t + 1],
+                )
 
         zp_planes = []
         for h in range(2):
@@ -224,7 +237,7 @@ def tile_picked_listsmooth_sigmoid_po_kernel(
                 nc.vector.tensor_tensor(
                     sums[:, t, :],
                     windows[t][:].indirect(nb_sb[:, 16 * h : 16 * h + 16]),
-                    plains[t][:, cols(h * HALF, HALF)],
+                    plains[t][h][:],
                     ALU.add,
                 )
             sig = new("sig%d" % h, [P, 4, HALF], F32)
@@ -235,20 +248,32 @@ def tile_picked_listsmooth_sigmoid_po_kernel(
             zp_planes.append(planes)
 
         zv_woven = sb.tile([P, 4 * W], BF16, name="zv_woven", tag="s_window3", align_bytes=64)
-        quantise(zv_c[:], zv_s[:], weave(nc.vector.tensor_copy, zv_woven[:], zv_planes))
+        for c in (2, 3):
+            acc = bank("zv_acc_v%d" % c)
+            for t in range(4):
+                mx(acc[:, cols(t * P, P)], *k_slot(t), wv_c[:, cols(c * P, P)].bitcast(FP8X4), wv_s[:, cols(c * P, P)])
+            nc.vector.tensor_tensor(
+                zv_woven[:].rearrange("p (u m t) -> p u m t", u=4, t=4)[:, :, 32 * c : 32 * c + 32],
+                acc[:].rearrange("p (t m u) -> p u m t", t=4, u=4),
+                gi_c.unsqueeze(1).unsqueeze(1).to_broadcast([P, 4, 32, 4]),
+                ALU.mult,
+            )
+        nc.vector.tensor_copy(
+            zv_woven[:].rearrange("p (u c i t) -> p u c t i", u=4, i=4, t=4)[:, :, 0:16],
+            zv_planes[:].rearrange("p t (u c i) -> p u c t i", u=4, i=4),
+        )
+        zp_woven = [sb.tile([P, 4 * HALF], BF16, name="zp_woven%d" % h, tag="zp_woven%d" % h, align_bytes=64) for h in range(2)]
+        zp = [(new("zp_c%d" % h, [P, HALF], U32), new("zp_s%d" % h, [P, HALF], U8)) for h in range(2)]
+        weave(nc.vector.tensor_copy, zp_woven[0][:], zp_planes[0])
+        quantise(zv_c[:], zv_s[:], zv_woven[:])
+        quantise(zp[0][0][:], zp[0][1][:], zp_woven[0][:])
+        weave(nc.vector.tensor_copy, zp_woven[1][:], zp_planes[1])
+        quantise(zp[1][0][:], zp[1][1][:], zp_woven[1][:])
 
         y_s = new("y_s", [P, W], U8)
         out_rows = out_0.rearrange("(p t) v -> p t v", t=4)
         out_words = out_1[0].rearrange("p n t -> p (n t)").bitcast(I32)
-        zp = []
-        for h in range(2):
-            woven = new("zp_woven%d" % h, [P, 4 * HALF], BF16)
-            woven = weave(nc.vector.tensor_copy, woven[:], zp_planes[h])
-            zp_c = new("zp_c%d" % h, [P, HALF], U32)
-            zp_s = new("zp_s%d" % h, [P, HALF], U8)
-            quantise(zp_c[:], zp_s[:], woven)
-            zp.append((zp_c, zp_s))
-        y_woven = []
+        y_half = [new("y_woven%d" % h, [P, 4 * HALF], BF16) for h in range(2)]
         for c in range(4):
             zp_c, zp_s = zp[c // 2]
             part = cols((c % 2) * P, P)
@@ -261,16 +286,15 @@ def tile_picked_listsmooth_sigmoid_po_kernel(
                     zp_c[:, part].bitcast(FP8X4),
                     zp_s[:, part],
                 )
-            y = new("y%d" % c, [P, 4, P], F32)
+            y = sb.tile([P, 4, P], F32, name="y%d" % c, tag="zp_woven1" if c == 0 else "y%d" % c, align_bytes=64)
             nc.vector.scalar_tensor_tensor(
                 y[:], acc[:].rearrange("p (t n) -> p t n", t=4), SIXTEENTH, res_sb[:, :, cols(c * P, P)], ALU.mult, ALU.add
             )
             nc.sync.dma_start(out_rows[:, :, cols(c * P, P)], y[:])
-            woven = new("y_woven%d" % c, [P, 4 * P], BF16)
-            y_woven.append(weave(nc.vector.tensor_copy if c == 3 else nc.scalar.copy, woven[:], y))
-        for c in range(4):
-            y_c = new("y_c%d" % c, [P, P], U32)
-            quantise(y_c[:], y_s[:, cols(c * P, P)], y_woven[c])
-            nc.sync.dma_start(out_words[:, cols(c * P, P)], y_c[:].bitcast(I32))
+            weave(nc.vector.tensor_copy if c == 3 else nc.scalar.copy, y_half[c // 2][:, cols((c % 2) * 4 * P, 4 * P)], y)
+        for h in range(2):
+            y_c = new("y_c%d" % h, [P, HALF], U32)
+            quantise(y_c[:], y_s[:, cols(h * HALF, HALF)], y_half[h][:])
+            nc.sync.dma_start(out_words[:, cols(h * HALF, HALF)], y_c[:].bitcast(I32))
         for q in range(4):
             (nc.scalar if q % 2 else nc.sync).dma_start(out_2[0, 4 * q : 4 * q + 4, :].bitcast(I32), y_s[32 * q : 32 * q + 4, :].bitcast(I32))

@@ -32,8 +32,8 @@ def tile_picked_listsmooth_sigmoid_po_kernel(
         sb = ctx.enter_context(tc.tile_pool(name="sb", bufs=1))
         psum = ctx.enter_context(tc.psum_pool(name="psum", bufs=8))
 
-        def new(name, shape, dtype):
-            return sb.tile(shape, dtype, name=name, align_bytes=64)
+        def new(name, shape, dtype, over=None):
+            return sb.tile(shape, dtype, name=name, tag=over or name, align_bytes=64)
 
         def bank(name):
             return psum.tile([P, W], F32, name=name, tag="bank")
@@ -43,7 +43,7 @@ def tile_picked_listsmooth_sigmoid_po_kernel(
         nb_sb = lists.tile([P, W // 16], U16, name="nb_sb")
         xs = new("xs", [P, T], U8)
         xw = sb.tile([P, T], I32, name="xw", tag="xw_then_res", align_bytes=64)
-        nc.gpsimd.memset(xs[:].bitcast(I32), 0)
+        nc.vector.memset(xs[:].bitcast(I32), 0)
         w_raw_s = [new("w%d_raw_s" % j, [P, W], U8) for j in (2, 1)]
         for raw_s in w_raw_s:
             nc.vector.memset(raw_s[:].bitcast(I32), 0)
@@ -89,11 +89,11 @@ def tile_picked_listsmooth_sigmoid_po_kernel(
         g_cols = new("g_cols", [P, 16], F32)
         nc.scalar.copy(g_cols[:], g_ps[:, 0:16])
         gq_c, gk_c, gi_c, gt_c = [g_cols[:, 4 * j : 4 * j + 4] for j in range(4)]
+        w1_raw = (load_words("w1", w1_words), load_scales(w1_scales, w_raw_s[1]))
         wv_rows = wv.rearrange("(p j) c -> p j c", j=4)
-        wv_raw = [sb.tile([P, 4, HALF], F32, name="wv_raw%d" % h, tag="wv_raw%d" % h, align_bytes=64) for h in range(2)]
+        wv_raw = [new("wv_raw%d" % h, [P, 4, HALF], F32) for h in range(2)]
         for h in range(2):
             nc.sync.dma_start(wv_raw[h][:], wv_rows[:, :, h * HALF : (h + 1) * HALF])
-        w1_raw = (load_words("w1", w1_words), load_scales(w1_scales, w_raw_s[1]))
         nc.sync.dma_start(nb_sb[:], nb)
 
         def deal(engine, name, raw, width):
@@ -104,24 +104,23 @@ def tile_picked_listsmooth_sigmoid_po_kernel(
             )
             return dealt
 
+        w2_w = deal(nc.vector, "w2_w", w2_raw[0], 2 * W)
         q_scale = new("q_scale", [P, W], U8)
         nc.vector.tensor_copy(q_scale[:], xs[:].indirect(qs_sb[:]))
         k_scale_raw = new("k_scale_raw", [P, W], U8)
         nc.vector.tensor_copy(k_scale_raw[:], xs[:].indirect(offs_sb[:]))
         k_scale = deal(nc.vector, "k_scale", k_scale_raw, W)
-        w2_w = deal(nc.gpsimd, "w2_w", w2_raw[0], 2 * W)
-        w2_s = deal(nc.gpsimd, "w2_s", w2_raw[1], W)
-        q_words = []
-        for h in range(2):
-            t_ = new("q_words%d" % h, [P, HALF], U32)
-            nc.vector.tensor_copy(t_[:], xw[:].bitcast(U32).indirect(qs_sb[:, 16 * h : 16 * h + 16]))
-            q_words.append(t_)
+        q_words = [new("q_words0", [P, HALF], U32)]
+        nc.vector.tensor_copy(q_words[0][:], xw[:].bitcast(U32).indirect(qs_sb[:, 0:16]))
+        w2_s = deal(nc.vector, "w2_s", w2_raw[1], W)
+        q_words.append(new("q_words1", [P, HALF], U32, over="w2_raw_s"))
+        nc.vector.tensor_copy(q_words[1][:], xw[:].bitcast(U32).indirect(qs_sb[:, 16:32]))
         k_words = new("k_words", [P, W], U32)
         nc.vector.tensor_copy(
             k_words[:].rearrange("p (t b r) -> p b t r", t=4, b=16), xw[:].bitcast(U32).indirect(offs_sb[:])
         )
-        w1_w = deal(nc.gpsimd, "w1_w", w1_raw[0], 2 * W)
-        w1_s = deal(nc.gpsimd, "w1_s", w1_raw[1], W)
+        w1_w = deal(nc.vector, "w1_w", w1_raw[0], 2 * W)
+        w1_s = deal(nc.vector, "w1_s", w1_raw[1], W)
 
         res_sb = sb.tile([P, 4, W], F32, name="res_sb", tag="xw_then_res", align_bytes=64)
         nc.sync.dma_start(res_sb[:], res.rearrange("(p t) v -> p t v", t=4))
@@ -144,8 +143,8 @@ def tile_picked_listsmooth_sigmoid_po_kernel(
         def quantise(codes, scales, woven):
             nc.vector.quantize_mx(out=codes.bitcast(FP8X4), scales=scales, in_=woven)
 
-        def scaled_planes(name, lhs_slot, rhs, rhs_s, n, g):
-            planes = new(name + "_planes", [P, 4, n], BF16)
+        def scaled_planes(name, lhs_slot, rhs, rhs_s, n, g, over=None):
+            planes = new(name + "_planes", [P, 4, n], BF16, over)
             per_bank = W // n
             for t0 in range(0, 4, per_bank):
                 acc = bank(name + "_acc%d" % t0)
@@ -180,23 +179,29 @@ def tile_picked_listsmooth_sigmoid_po_kernel(
         z2_s = new("z2_s", [P, W], U8)
         z_c = new("z_c", [P, W], U32)
         z_s = new("z_s", [P, W], U8)
-        wv_woven = new("wv_woven", [P, 4 * W], BF16)
-        weave(nc.vector.tensor_copy, wv_woven[:, 0 : 4 * HALF], wv_raw[0])
-        z2_woven = sb.tile([P, 4 * W], BF16, name="z2_woven", tag="wv_raw0", align_bytes=64)
+        z2_woven = new("z2_woven", [P, 4 * W], BF16, over="w1_raw_s")
         planes = scaled_planes("z2_0", w2_slot, q_words[0][:].bitcast(FP8X4), q_scale[:, 0:HALF], HALF, gq_c)
         for c in (2, 3):
             by_vector("z2_%d" % c, z2_woven[:, cols(4 * P * c, 4 * P)], w2_slot, q_words[1][:, cols((c - 2) * P, P)].bitcast(FP8X4), q_scale[:, cols(c * P, P)], gq_c)
         weave(nc.vector.tensor_copy, z2_woven[:, 0 : 4 * HALF], planes)
-        weave(nc.scalar.copy, wv_woven[:, 4 * HALF :], wv_raw[1])
         z_woven0 = new("z_woven0", [P, 4 * P], BF16)
         by_vector("z_0", z_woven0[:], w1_slot, k_words[:, 0:P].bitcast(FP8X4), k_scale[:, 0:P], gk_c)
         quantise(z2_c[:], z2_s[:], z2_woven[:])
         quantise(z_c[:, 0:P], z_s[:, 0:P], z_woven0[:])
         rest = []
         for c0, n in ((P, P), (HALF, HALF)):
-            planes = scaled_planes("z_%d" % c0, w1_slot, k_words[:, cols(c0, n)].bitcast(FP8X4), k_scale[:, cols(c0, n)], n, gk_c)
+            planes = scaled_planes("z_%d" % c0, w1_slot, k_words[:, cols(c0, n)].bitcast(FP8X4), k_scale[:, cols(c0, n)], n, gk_c, None)
             woven = new("z_woven%d" % c0, [P, 4 * n], BF16)
             rest.append((c0, n, weave(nc.vector.tensor_copy, woven[:], planes)))
+        wv_woven = new("wv_woven", [P, 4 * W], BF16)
+
+        def weave_wv(engine_copy, h):
+            engine_copy(
+                wv_woven[:].rearrange("p (t m j) -> p m j t", t=4, j=4)[:, 64 * h : 64 * h + 64],
+                wv_raw[h][:].rearrange("p j (m t) -> p m j t", t=4),
+            )
+
+        weave_wv(nc.scalar.copy, 0)
         for c0, n, woven in rest:
             quantise(z_c[:, cols(c0, n)], z_s[:, cols(c0, n)], woven)
 
@@ -212,23 +217,13 @@ def tile_picked_listsmooth_sigmoid_po_kernel(
             windows.append(window)
             plains.append(plain)
 
+        weave_wv(nc.vector.tensor_copy, 1)
         wv_c = new("wv_c", [P, W], U32)
         wv_s = new("wv_s", [P, W], U8)
         quantise(wv_c[:], wv_s[:], wv_woven[:])
         zv_c = new("zv_c", [P, W], U32)
         zv_s = new("zv_s", [P, W], U8)
-        zv_planes = new("zv_planes", [P, 4, HALF], BF16)
-        for t0 in (0, 2):
-            acc = bank("zv_acc%d" % t0)
-            for t in (t0, t0 + 1):
-                mx(acc[:, cols((t - t0) * HALF, HALF)], *k_slot(t), wv_c[:, 0:HALF].bitcast(FP8X4), wv_s[:, 0:HALF])
-            for t in (t0, t0 + 1):
-                nc.scalar.activation(
-                    zv_planes[:, t, :].rearrange("p (u m) -> p u m", u=4),
-                    acc[:, cols((t - t0) * HALF, HALF)].rearrange("p (m u) -> p u m", u=4),
-                    ACT.Copy,
-                    scale=gi_c[:, t : t + 1],
-                )
+        zv_planes = scaled_planes("zv", k_slot, wv_c[:, 0:HALF].bitcast(FP8X4), wv_s[:, 0:HALF], HALF, gi_c)
 
         zp_planes = []
         for h in range(2):
@@ -249,20 +244,9 @@ def tile_picked_listsmooth_sigmoid_po_kernel(
 
         zv_woven = sb.tile([P, 4 * W], BF16, name="zv_woven", tag="s_window3", align_bytes=64)
         for c in (2, 3):
-            acc = bank("zv_acc_v%d" % c)
-            for t in range(4):
-                mx(acc[:, cols(t * P, P)], *k_slot(t), wv_c[:, cols(c * P, P)].bitcast(FP8X4), wv_s[:, cols(c * P, P)])
-            nc.vector.tensor_tensor(
-                zv_woven[:].rearrange("p (u m t) -> p u m t", u=4, t=4)[:, :, 32 * c : 32 * c + 32],
-                acc[:].rearrange("p (t m u) -> p u m t", t=4, u=4),
-                gi_c.unsqueeze(1).unsqueeze(1).to_broadcast([P, 4, 32, 4]),
-                ALU.mult,
-            )
-        nc.vector.tensor_copy(
-            zv_woven[:].rearrange("p (u c i t) -> p u c t i", u=4, i=4, t=4)[:, :, 0:16],
-            zv_planes[:].rearrange("p t (u c i) -> p u c t i", u=4, i=4),
-        )
-        zp_woven = [sb.tile([P, 4 * HALF], BF16, name="zp_woven%d" % h, tag="zp_woven%d" % h, align_bytes=64) for h in range(2)]
+            by_vector("zv_%d" % c, zv_woven[:, cols(4 * P * c, 4 * P)], k_slot, wv_c[:, cols(c * P, P)].bitcast(FP8X4), wv_s[:, cols(c * P, P)], gi_c)
+        weave(nc.vector.tensor_copy, zv_woven[:, 0 : 4 * HALF], zv_planes)
+        zp_woven = [new("zp_woven%d" % h, [P, 4 * HALF], BF16) for h in range(2)]
         zp = [(new("zp_c%d" % h, [P, HALF], U32), new("zp_s%d" % h, [P, HALF], U8)) for h in range(2)]
         weave(nc.vector.tensor_copy, zp_woven[0][:], zp_planes[0])
         quantise(zv_c[:], zv_s[:], zv_woven[:])
@@ -286,7 +270,7 @@ def tile_picked_listsmooth_sigmoid_po_kernel(
                     zp_c[:, part].bitcast(FP8X4),
                     zp_s[:, part],
                 )
-            y = sb.tile([P, 4, P], F32, name="y%d" % c, tag="zp_woven1" if c == 0 else "y%d" % c, align_bytes=64)
+            y = new("y%d" % c, [P, 4, P], F32, "zp_woven1" if c == 0 else None)
             nc.vector.scalar_tensor_tensor(
                 y[:], acc[:].rearrange("p (t n) -> p t n", t=4), SIXTEENTH, res_sb[:, :, cols(c * P, P)], ALU.mult, ALU.add
             )

@@ -42,22 +42,24 @@ def tile_picked_listsmooth_sigmoid_po_kernel(
         offs_sb = lists.tile([P, W // 16], U16, name="offs_sb")
         nb_sb = lists.tile([P, W // 16], U16, name="nb_sb")
         xs = new("xs", [P, T], U8)
-        xw = sb.tile([P, T], I32, name="xw", tag="xw_then_res", align_bytes=64)
-        nc.vector.memset(xs[:].bitcast(I32), 0)
-        w_raw_s = [new("w%d_raw_s" % j, [P, W], U8) for j in (2, 1)]
+        xw = new("xw", [P, T], I32)
+        nc.gpsimd.memset(xs[:].bitcast(I32), 0)
+        w_raw_s = [new("w2_raw_s", [P, W], U8), new("w1_raw_s", [P, W], U8)]
         for raw_s in w_raw_s:
             nc.vector.memset(raw_s[:].bitcast(I32), 0)
-        g_rows = new("g_rows", [P, P], F32)
-        nc.gpsimd.memset(g_rows[:], 0.0)
+        g_rows = [new("g_rows%d" % j, [P, P], F32) for j in range(3)]
+        for rows in g_rows:
+            nc.vector.memset(rows[:], 0.0)
         warm_in = new("warm_in", [P, 1], F32)
         nc.vector.memset(warm_in[:], 0.0)
         warm = new("warm", [P, 1], F32)
         nc.scalar.activation(warm[:], warm_in[:], ACT.Sigmoid)
 
         nc.sync.dma_start(qs_sb[:], qs)
-        nc.sync.dma_start(offs_sb[:], offs)
         for q in range(4):
             nc.sync.dma_start(xs[32 * q : 32 * q + 4, :].bitcast(I32), x_scales[0, 4 * q : 4 * q + 4, :].bitcast(I32))
+
+        nc.sync.dma_start(offs_sb[:], offs)
 
         def load_words(name, words):
             raw_w = new(name + "_raw_w", [P, 2 * W], U8)
@@ -69,32 +71,36 @@ def tile_picked_listsmooth_sigmoid_po_kernel(
                 nc.sync.dma_start(raw_s[32 * q : 32 * q + 4, :].bitcast(I32), scales[0, 4 * q : 4 * q + 4, :].bitcast(I32))
             return raw_s
 
-        def load_factor(engine, j, g):
+        def load_factor(engine, rows, j, g):
             engine.dma_start(
-                g_rows[4 * j : 4 * j + 4, :].rearrange("t (b r) -> t b r", r=8),
+                rows[4 * j : 4 * j + 4, :].rearrange("t (b r) -> t b r", r=8),
                 g.rearrange("(b t r) o -> t b (r o)", t=4, r=8),
             )
 
-        w2_raw_w = load_words("w2", w2_words)
+        def turn(name, rows, n):
+            g_ps = bank(name + "_ps")
+            nc.tensor.transpose(g_ps[:, 0:P], rows[:], ident[:])
+            g_cols = new(name, [P, n], F32)
+            nc.scalar.copy(g_cols[:], g_ps[:, 0:n])
+            return g_cols
+
+        load_factor(nc.sync, g_rows[0], 0, gq)
         nc.sync.dma_start(xw[:], x_words[0].rearrange("p n t -> p (n t)").bitcast(I32))
+        w2_raw_w = load_words("w2", w2_words)
         w2_raw = (w2_raw_w, load_scales(w2_scales, w_raw_s[0]))
-        load_factor(nc.sync, 0, gq)
-        load_factor(nc.sync, 1, gk)
-        load_factor(nc.gpsimd, 2, gi)
-        load_factor(nc.gpsimd, 3, gt)
+        load_factor(nc.sync, g_rows[1], 0, gk)
         ident = new("ident", [P, P], F32)
         make_identity(nc, ident[:])
-        g_ps = bank("g_ps")
-        nc.tensor.transpose(g_ps[:, 0:P], g_rows[:], ident[:])
-        g_cols = new("g_cols", [P, 16], F32)
-        nc.scalar.copy(g_cols[:], g_ps[:, 0:16])
-        gq_c, gk_c, gi_c, gt_c = [g_cols[:, 4 * j : 4 * j + 4] for j in range(4)]
+        gq_c = turn("gq_cols", g_rows[0], 4)[:, 0:4]
+        gk_c = turn("gk_cols", g_rows[1], 4)[:, 0:4]
         w1_raw = (load_words("w1", w1_words), load_scales(w1_scales, w_raw_s[1]))
+        nc.sync.dma_start(nb_sb[:], nb)
         wv_rows = wv.rearrange("(p j) c -> p j c", j=4)
         wv_raw = [new("wv_raw%d" % h, [P, 4, HALF], F32) for h in range(2)]
         for h in range(2):
             nc.sync.dma_start(wv_raw[h][:], wv_rows[:, :, h * HALF : (h + 1) * HALF])
-        nc.sync.dma_start(nb_sb[:], nb)
+        load_factor(nc.sync, g_rows[2], 0, gi)
+        load_factor(nc.sync, g_rows[2], 1, gt)
 
         def deal(engine, name, raw, width):
             dealt = new(name, [P, width], U8)
@@ -104,26 +110,26 @@ def tile_picked_listsmooth_sigmoid_po_kernel(
             )
             return dealt
 
-        w2_w = deal(nc.vector, "w2_w", w2_raw[0], 2 * W)
+        res_sb = new("res_sb", [P, 4, W], F32)
+        nc.sync.dma_start(res_sb[:], res.rearrange("(p t) v -> p t v", t=4))
+
         q_scale = new("q_scale", [P, W], U8)
         nc.vector.tensor_copy(q_scale[:], xs[:].indirect(qs_sb[:]))
         k_scale_raw = new("k_scale_raw", [P, W], U8)
         nc.vector.tensor_copy(k_scale_raw[:], xs[:].indirect(offs_sb[:]))
-        k_scale = deal(nc.vector, "k_scale", k_scale_raw, W)
         q_words = [new("q_words0", [P, HALF], U32)]
         nc.vector.tensor_copy(q_words[0][:], xw[:].bitcast(U32).indirect(qs_sb[:, 0:16]))
-        w2_s = deal(nc.vector, "w2_s", w2_raw[1], W)
-        q_words.append(new("q_words1", [P, HALF], U32, over="w2_raw_s"))
+        w2_w = deal(nc.gpsimd, "w2_w", w2_raw[0], 2 * W)
+        w2_s = deal(nc.gpsimd, "w2_s", w2_raw[1], W)
+        q_words.append(new("q_words1", [P, HALF], U32))
         nc.vector.tensor_copy(q_words[1][:], xw[:].bitcast(U32).indirect(qs_sb[:, 16:32]))
         k_words = new("k_words", [P, W], U32)
         nc.vector.tensor_copy(
             k_words[:].rearrange("p (t b r) -> p b t r", t=4, b=16), xw[:].bitcast(U32).indirect(offs_sb[:])
         )
-        w1_w = deal(nc.vector, "w1_w", w1_raw[0], 2 * W)
-        w1_s = deal(nc.vector, "w1_s", w1_raw[1], W)
-
-        res_sb = sb.tile([P, 4, W], F32, name="res_sb", tag="xw_then_res", align_bytes=64)
-        nc.sync.dma_start(res_sb[:], res.rearrange("(p t) v -> p t v", t=4))
+        k_scale = deal(nc.vector, "k_scale", k_scale_raw, W)
+        w1_w = deal(nc.gpsimd, "w1_w", w1_raw[0], 2 * W)
+        w1_s = deal(nc.gpsimd, "w1_s", w1_raw[1], W)
 
         def mx(out, lhs, lhs_s, rhs, rhs_s):
             nc.tensor.matmul_mx(out=out, lhsT=lhs, lhsT_scale=lhs_s, rhs=rhs, rhs_scale=rhs_s, start=True, stop=True)
@@ -179,20 +185,18 @@ def tile_picked_listsmooth_sigmoid_po_kernel(
         z2_s = new("z2_s", [P, W], U8)
         z_c = new("z_c", [P, W], U32)
         z_s = new("z_s", [P, W], U8)
-        z2_woven = new("z2_woven", [P, 4 * W], BF16, over="w1_raw_s")
-        planes = scaled_planes("z2_0", w2_slot, q_words[0][:].bitcast(FP8X4), q_scale[:, 0:HALF], HALF, gq_c)
-        for c in (2, 3):
-            by_vector("z2_%d" % c, z2_woven[:, cols(4 * P * c, 4 * P)], w2_slot, q_words[1][:, cols((c - 2) * P, P)].bitcast(FP8X4), q_scale[:, cols(c * P, P)], gq_c)
-        weave(nc.vector.tensor_copy, z2_woven[:, 0 : 4 * HALF], planes)
-        z_woven0 = new("z_woven0", [P, 4 * P], BF16)
-        by_vector("z_0", z_woven0[:], w1_slot, k_words[:, 0:P].bitcast(FP8X4), k_scale[:, 0:P], gk_c)
+        z2_woven = new("z2_woven", [P, 4 * W], BF16)
+        planes0 = scaled_planes("z2_0", w2_slot, q_words[0][:].bitcast(FP8X4), q_scale[:, 0:HALF], HALF, gq_c)
+        planes2 = scaled_planes("z2_2", w2_slot, q_words[1][:, 0:P].bitcast(FP8X4), q_scale[:, cols(HALF, P)], P, gq_c)
+        by_vector("z2_3", z2_woven[:, cols(4 * P * 3, 4 * P)], w2_slot, q_words[1][:, cols(P, P)].bitcast(FP8X4), q_scale[:, cols(3 * P, P)], gq_c)
+        weave(nc.vector.tensor_copy, z2_woven[:, 0 : 4 * HALF], planes0)
+        weave(nc.vector.tensor_copy, z2_woven[:, cols(4 * HALF, 4 * P)], planes2)
         quantise(z2_c[:], z2_s[:], z2_woven[:])
-        quantise(z_c[:, 0:P], z_s[:, 0:P], z_woven0[:])
-        rest = []
-        for c0, n in ((P, P), (HALF, HALF)):
-            planes = scaled_planes("z_%d" % c0, w1_slot, k_words[:, cols(c0, n)].bitcast(FP8X4), k_scale[:, cols(c0, n)], n, gk_c, None)
-            woven = new("z_woven%d" % c0, [P, 4 * n], BF16)
-            rest.append((c0, n, weave(nc.vector.tensor_copy, woven[:], planes)))
+        for c0 in (0, HALF):
+            planes = scaled_planes("z_%d" % c0, w1_slot, k_words[:, cols(c0, HALF)].bitcast(FP8X4), k_scale[:, cols(c0, HALF)], HALF, gk_c)
+            woven = new("z_woven%d" % c0, [P, 4 * HALF], BF16)
+            weave(nc.vector.tensor_copy, woven[:], planes)
+            quantise(z_c[:, cols(c0, HALF)], z_s[:, cols(c0, HALF)], woven[:])
         wv_woven = new("wv_woven", [P, 4 * W], BF16)
 
         def weave_wv(engine_copy, h):
@@ -202,21 +206,21 @@ def tile_picked_listsmooth_sigmoid_po_kernel(
             )
 
         weave_wv(nc.scalar.copy, 0)
-        for c0, n, woven in rest:
-            quantise(z_c[:, cols(c0, n)], z_s[:, cols(c0, n)], woven)
 
-        windows, plains = [], []
+        windows = [new("s_window%d" % t, [P, 2 * W if t else W], F32) for t in range(4)]
+        plain3 = new("s_plain3", [P, W], F32)
+        plains = [windows[t + 1][:, W:] for t in range(3)] + [plain3[:]]
         for t in range(4):
             acc = bank("s_acc%d" % t)
             mx(acc[:], z_c[:, cols(t * P, P)].bitcast(FP8X4), z_s[:, cols(t * P, P)], z2_c[:].bitcast(FP8X4), z2_s[:])
-            window = sb.tile([P, W], F32, name="s_window%d" % t, tag="s_window%d" % t, align_bytes=64)
-            plain = [new("s_plain%d_%d" % (t, h), [P, HALF], F32) for h in range(2)]
-            nc.scalar.activation(window[:], acc[:], ACT.Copy, scale=SIXTEENTH)
-            nc.scalar.activation(plain[0][:], acc[:, 0:HALF], ACT.Copy, scale=SIXTEENTH)
-            nc.sync.dma_start(plain[1][:], window[:, HALF:])
-            windows.append(window)
-            plains.append(plain)
+            nc.scalar.activation(windows[t][:, 0:W], acc[:], ACT.Copy, scale=SIXTEENTH)
+            if t < 2:
+                nc.scalar.activation(plains[t], acc[:], ACT.Copy, scale=SIXTEENTH)
+            else:
+                nc.sync.dma_start(plains[t], windows[t][:, 0:W])
 
+        g_cols = turn("g_cols", g_rows[2], 8)
+        gi_c, gt_c = g_cols[:, 0:4], g_cols[:, 4:8]
         weave_wv(nc.vector.tensor_copy, 1)
         wv_c = new("wv_c", [P, W], U32)
         wv_s = new("wv_s", [P, W], U8)
@@ -225,42 +229,54 @@ def tile_picked_listsmooth_sigmoid_po_kernel(
         zv_s = new("zv_s", [P, W], U8)
         zv_planes = scaled_planes("zv", k_slot, wv_c[:, 0:HALF].bitcast(FP8X4), wv_s[:, 0:HALF], HALF, gi_c)
 
-        zp_planes = []
-        for h in range(2):
-            sums = new("sums%d" % h, [P, 4, HALF], F32)
-            for t in range(4):
-                nc.vector.tensor_tensor(
-                    sums[:, t, :],
-                    windows[t][:].indirect(nb_sb[:, 16 * h : 16 * h + 16]),
-                    plains[t][h][:],
-                    ALU.add,
-                )
-            sig = new("sig%d" % h, [P, 4, HALF], F32)
-            nc.scalar.activation(sig[:], sums[:], ACT.Sigmoid)
-            planes = new("zp_planes%d" % h, [P, 4, HALF], BF16)
-            for t in range(4):
-                nc.scalar.activation(planes[:, t, :], sig[:, t, :], ACT.Copy, scale=gt_c[:, t : t + 1])
-            zp_planes.append(planes)
+        sums = new("sums", [P, 4, W], F32)
+        sig = new("sig", [P, 4, W], F32)
+        zp_planes = [new("zp_planes%d" % h, [P, 4, HALF], BF16) for h in range(2)]
 
-        zv_woven = sb.tile([P, 4 * W], BF16, name="zv_woven", tag="s_window3", align_bytes=64)
+        def smooth(t, c0, n):
+            nc.vector.tensor_tensor(
+                sums[:, t, cols(c0, n)], windows[t][:].indirect(nb_sb[:, c0 // 16 : (c0 + n) // 16]), plains[t][:, cols(c0, n)], ALU.add
+            )
+
+        def gate(t, c0, n):
+            nc.scalar.activation(sig[:, t, cols(c0, n)], sums[:, t, cols(c0, n)], ACT.Sigmoid)
+            for h in range(c0 // HALF, (c0 + n) // HALF):
+                nc.scalar.activation(zp_planes[h][:, t, :], sig[:, t, cols(h * HALF, HALF)], ACT.Copy, scale=gt_c[:, t : t + 1])
+
+        smooth(0, 0, HALF)
+        smooth(0, HALF, HALF)
+        gate(0, 0, W)
+        smooth(1, 0, W)
+        gate(1, 0, W)
+        zv_woven1 = new("zv_woven1", [P, 4 * HALF], BF16)
         for c in (2, 3):
-            by_vector("zv_%d" % c, zv_woven[:, cols(4 * P * c, 4 * P)], k_slot, wv_c[:, cols(c * P, P)].bitcast(FP8X4), wv_s[:, cols(c * P, P)], gi_c)
-        weave(nc.vector.tensor_copy, zv_woven[:, 0 : 4 * HALF], zv_planes)
+            by_vector("zv_%d" % c, zv_woven1[:, cols(4 * P * (c - 2), 4 * P)], k_slot, wv_c[:, cols(c * P, P)].bitcast(FP8X4), wv_s[:, cols(c * P, P)], gi_c)
+        quantise(zv_c[:, HALF:], zv_s[:, HALF:], zv_woven1[:])
+        smooth(2, 0, W)
+        gate(2, 0, W)
+        for h in range(2):
+            smooth(3, h * HALF, HALF)
+            gate(3, h * HALF, HALF)
+
+        zv_woven0 = new("zv_woven0", [P, 4 * HALF], BF16, over="s_plain3")
+        weave(nc.vector.tensor_copy, zv_woven0[:], zv_planes)
         zp_woven = [new("zp_woven%d" % h, [P, 4 * HALF], BF16) for h in range(2)]
-        zp = [(new("zp_c%d" % h, [P, HALF], U32), new("zp_s%d" % h, [P, HALF], U8)) for h in range(2)]
         weave(nc.vector.tensor_copy, zp_woven[0][:], zp_planes[0])
-        quantise(zv_c[:], zv_s[:], zv_woven[:])
-        quantise(zp[0][0][:], zp[0][1][:], zp_woven[0][:])
-        weave(nc.vector.tensor_copy, zp_woven[1][:], zp_planes[1])
-        quantise(zp[1][0][:], zp[1][1][:], zp_woven[1][:])
+        weave(nc.scalar.copy, zp_woven[1][:], zp_planes[1])
+        quantise(zv_c[:, 0:HALF], zv_s[:, 0:HALF], zv_woven0[:])
+        zp = []
+        for h in range(2):
+            zp_c = new("zp_c%d" % h, [P, HALF], U32)
+            zp_s = new("zp_s%d" % h, [P, HALF], U8)
+            quantise(zp_c[:], zp_s[:], zp_woven[h][:])
+            zp.extend((zp_c, zp_s, cols(j, P)) for j in (0, P))
 
         y_s = new("y_s", [P, W], U8)
         out_rows = out_0.rearrange("(p t) v -> p t v", t=4)
         out_words = out_1[0].rearrange("p n t -> p (n t)").bitcast(I32)
         y_half = [new("y_woven%d" % h, [P, 4 * HALF], BF16) for h in range(2)]
         for c in range(4):
-            zp_c, zp_s = zp[c // 2]
-            part = cols((c % 2) * P, P)
+            zp_c, zp_s, part = zp[c]
             acc = bank("out_acc%d" % c)
             for t in range(4):
                 mx(
@@ -270,7 +286,7 @@ def tile_picked_listsmooth_sigmoid_po_kernel(
                     zp_c[:, part].bitcast(FP8X4),
                     zp_s[:, part],
                 )
-            y = new("y%d" % c, [P, 4, P], F32, "zp_woven1" if c == 0 else None)
+            y = new("y%d" % c, [P, 4, P], F32)
             nc.vector.scalar_tensor_tensor(
                 y[:], acc[:].rearrange("p (t n) -> p t n", t=4), SIXTEENTH, res_sb[:, :, cols(c * P, P)], ALU.mult, ALU.add
             )

@@ -102,8 +102,8 @@ def tile_picked_listsmooth_sigmoid_po_kernel(
         load_factor(nc.sync, g_rows[2], 0, gi)
         load_factor(nc.sync, g_rows[2], 1, gt)
 
-        def deal(engine, name, raw, width):
-            dealt = new(name, [P, width], U8)
+        def deal(engine, name, raw, width, over=None):
+            dealt = new(name, [P, width], U8, over)
             engine.tensor_copy(
                 dealt[:].bitcast(I32).rearrange("p (t b u) -> p t b u", t=4, b=16),
                 raw[:].bitcast(I32).rearrange("p (b t u) -> p t b u", t=4, b=16),
@@ -127,7 +127,7 @@ def tile_picked_listsmooth_sigmoid_po_kernel(
         nc.vector.tensor_copy(
             k_words[:].rearrange("p (t b r) -> p b t r", t=4, b=16), xw[:].bitcast(U32).indirect(offs_sb[:])
         )
-        k_scale = deal(nc.vector, "k_scale", k_scale_raw, W)
+        k_scale = deal(nc.vector, "k_scale", k_scale_raw, W, "w2_raw_w")
         w1_w = deal(nc.gpsimd, "w1_w", w1_raw[0], 2 * W)
         w1_s = deal(nc.gpsimd, "w1_s", w1_raw[1], W)
 
@@ -142,7 +142,7 @@ def tile_picked_listsmooth_sigmoid_po_kernel(
 
         def weave(engine_copy, woven, planes):
             engine_copy(
-                woven.rearrange("p (c i t) -> p c t i", i=4, t=4), planes[:].rearrange("p t (c i) -> p c t i", i=4)
+                woven.rearrange("p (c i t) -> p c t i", i=4, t=4), planes.rearrange("p t (c i) -> p c t i", i=4)
             )
             return woven
 
@@ -158,7 +158,7 @@ def tile_picked_listsmooth_sigmoid_po_kernel(
                     mx(acc[:, cols((t - t0) * n, n)], *lhs_slot(t), rhs, rhs_s)
                 for t in range(t0, t0 + per_bank):
                     nc.scalar.activation(planes[:, t, :], acc[:, cols((t - t0) * n, n)], ACT.Copy, scale=g[:, t : t + 1])
-            return planes
+            return planes[:]
 
         def by_vector(name, woven, lhs_slot, rhs, rhs_s, g):
             acc = bank(name + "_acc")
@@ -225,13 +225,12 @@ def tile_picked_listsmooth_sigmoid_po_kernel(
         wv_c = new("wv_c", [P, W], U32)
         wv_s = new("wv_s", [P, W], U8)
         quantise(wv_c[:], wv_s[:], wv_woven[:])
-        zv_c = new("zv_c", [P, W], U32)
         zv_s = new("zv_s", [P, W], U8)
         zv_planes = scaled_planes("zv", k_slot, wv_c[:, 0:HALF].bitcast(FP8X4), wv_s[:, 0:HALF], HALF, gi_c)
 
         sums = new("sums", [P, 4, W], F32)
         sig = new("sig", [P, 4, W], F32)
-        zp_planes = [new("zp_planes%d" % h, [P, 4, HALF], BF16) for h in range(2)]
+        zp_planes = new("zp_planes", [P, 2, 4, HALF], BF16)
 
         def smooth(t, c0, n):
             nc.vector.tensor_tensor(
@@ -240,32 +239,37 @@ def tile_picked_listsmooth_sigmoid_po_kernel(
 
         def gate(t, c0, n):
             nc.scalar.activation(sig[:, t, cols(c0, n)], sums[:, t, cols(c0, n)], ACT.Sigmoid)
-            for h in range(c0 // HALF, (c0 + n) // HALF):
-                nc.scalar.activation(zp_planes[h][:, t, :], sig[:, t, cols(h * HALF, HALF)], ACT.Copy, scale=gt_c[:, t : t + 1])
+            nc.scalar.activation(
+                zp_planes[:, c0 // HALF : (c0 + n) // HALF, t, :],
+                sig[:, t, cols(c0, n)].rearrange("p (h c) -> p h c", c=HALF),
+                ACT.Copy,
+                scale=gt_c[:, t : t + 1],
+            )
 
         smooth(0, 0, HALF)
         smooth(0, HALF, HALF)
         gate(0, 0, W)
         smooth(1, 0, W)
         gate(1, 0, W)
-        zv_woven1 = new("zv_woven1", [P, 4 * HALF], BF16)
+        zv_woven = new("zv_woven", [P, 4 * W], BF16)
         for c in (2, 3):
-            by_vector("zv_%d" % c, zv_woven1[:, cols(4 * P * (c - 2), 4 * P)], k_slot, wv_c[:, cols(c * P, P)].bitcast(FP8X4), wv_s[:, cols(c * P, P)], gi_c)
-        quantise(zv_c[:, HALF:], zv_s[:, HALF:], zv_woven1[:])
+            by_vector("zv_%d" % c, zv_woven[:, cols(4 * P * c, 4 * P)], k_slot, wv_c[:, cols(c * P, P)].bitcast(FP8X4), wv_s[:, cols(c * P, P)], gi_c)
+        weave(nc.vector.tensor_copy, zv_woven[:, 0 : 4 * HALF], zv_planes)
         smooth(2, 0, W)
         gate(2, 0, W)
         for h in range(2):
             smooth(3, h * HALF, HALF)
             gate(3, h * HALF, HALF)
 
-        zv_woven0 = new("zv_woven0", [P, 4 * HALF], BF16, over="s_plain3")
-        weave(nc.vector.tensor_copy, zv_woven0[:], zv_planes)
+        zv_c = new("zv_c", [P, W], U32, over="s_plain3")
+        quantise(zv_c[:], zv_s[:], zv_woven[:])
         zp_woven = [new("zp_woven%d" % h, [P, 4 * HALF], BF16) for h in range(2)]
-        weave(nc.vector.tensor_copy, zp_woven[0][:], zp_planes[0])
-        weave(nc.scalar.copy, zp_woven[1][:], zp_planes[1])
-        quantise(zv_c[:, 0:HALF], zv_s[:, 0:HALF], zv_woven0[:])
+        weave(nc.vector.tensor_copy, zp_woven[0][:], zp_planes[:, 0])
+        weave(nc.scalar.copy, zp_woven[1][:, 0 : 4 * P], zp_planes[:, 1, :, 0:P])
         zp = []
         for h in range(2):
+            if h == 1:
+                weave(nc.vector.tensor_copy, zp_woven[1][:, 4 * P :], zp_planes[:, 1, :, P:])
             zp_c = new("zp_c%d" % h, [P, HALF], U32)
             zp_s = new("zp_s%d" % h, [P, HALF], U8)
             quantise(zp_c[:], zp_s[:], zp_woven[h][:])
@@ -286,12 +290,12 @@ def tile_picked_listsmooth_sigmoid_po_kernel(
                     zp_c[:, part].bitcast(FP8X4),
                     zp_s[:, part],
                 )
-            y = new("y%d" % c, [P, 4, P], F32)
+            y = new("y%d" % c, [P, 4, P], F32, "zp_woven1" if c == 0 else None)
             nc.vector.scalar_tensor_tensor(
                 y[:], acc[:].rearrange("p (t n) -> p t n", t=4), SIXTEENTH, res_sb[:, :, cols(c * P, P)], ALU.mult, ALU.add
             )
             nc.sync.dma_start(out_rows[:, :, cols(c * P, P)], y[:])
-            weave(nc.vector.tensor_copy if c == 3 else nc.scalar.copy, y_half[c // 2][:, cols((c % 2) * 4 * P, 4 * P)], y)
+            weave(nc.vector.tensor_copy if c == 3 else nc.scalar.copy, y_half[c // 2][:, cols((c % 2) * 4 * P, 4 * P)], y[:])
         for h in range(2):
             y_c = new("y_c%d" % h, [P, HALF], U32)
             quantise(y_c[:], y_s[:, cols(h * HALF, HALF)], y_half[h][:])

@@ -3,7 +3,6 @@ from contextlib import ExitStack
 import concourse.mybir as mybir
 from concourse.masks import make_identity
 
-K, T, S, V, N, H = 512, 2048, 512, 512, 512, 512
 FLOPS = 5 * 2 * 512 * 512 * 512
 
 F32 = mybir.dt.float32
@@ -18,8 +17,10 @@ ACT = mybir.ActivationFunctionType
 ALU = mybir.AluOpType
 
 P = 128
+T = 2048
 W = 512
-HALF = 256
+HALF = W // 2
+ENTRIES = 16
 SIXTEENTH = 0.0625
 
 
@@ -38,69 +39,74 @@ def tile_picked_listsmooth_sigmoid_po_kernel(
         def bank(name):
             return psum.tile([P, W], F32, name=name, tag="bank")
 
-        qs_sb = lists.tile([P, W // 16], U16, name="qs_sb")
-        offs_sb = lists.tile([P, W // 16], U16, name="offs_sb")
-        nb_sb = lists.tile([P, W // 16], U16, name="nb_sb")
+        def cols(c0, n):
+            return slice(c0, c0 + n)
+
+        def entries(offsets, c0, n):
+            return offsets[:, c0 // ENTRIES : (c0 + n) // ENTRIES]
+
+        qs_sb = lists.tile([P, W // ENTRIES], U16, name="qs_sb")
+        offs_sb = lists.tile([P, W // ENTRIES], U16, name="offs_sb")
+        nb_sb = lists.tile([P, W // ENTRIES], U16, name="nb_sb")
         xs = new("xs", [P, T], U8)
         xw = new("xw", [P, T], I32)
         nc.gpsimd.memset(xs[:].bitcast(I32), 0)
-        w_raw_s = [new("w2_raw_s", [P, W], U8), new("w1_raw_s", [P, W], U8)]
-        for raw_s in w_raw_s:
+        w2_raw_s, w1_raw_s = new("w2_raw_s", [P, W], U8), new("w1_raw_s", [P, W], U8)
+        for raw_s in (w2_raw_s, w1_raw_s):
             nc.vector.memset(raw_s[:].bitcast(I32), 0)
-        g_rows = [new("g_rows%d" % j, [P, P], F32) for j in range(3)]
-        for rows in g_rows:
+        gq_rows, gk_rows, token_rows = [new("g_rows%d" % j, [P, P], F32) for j in range(3)]
+        for rows in (gq_rows, gk_rows, token_rows):
             nc.vector.memset(rows[:], 0.0)
         warm_in = new("warm_in", [P, 1], F32)
         nc.vector.memset(warm_in[:], 0.0)
         warm = new("warm", [P, 1], F32)
         nc.scalar.activation(warm[:], warm_in[:], ACT.Sigmoid)
 
-        nc.sync.dma_start(qs_sb[:], qs)
-        for q in range(4):
-            nc.sync.dma_start(xs[32 * q : 32 * q + 4, :].bitcast(I32), x_scales[0, 4 * q : 4 * q + 4, :].bitcast(I32))
+        def load_scales(tile, scales):
+            for q in range(4):
+                nc.sync.dma_start(tile[32 * q : 32 * q + 4, :].bitcast(I32), scales[0, 4 * q : 4 * q + 4, :].bitcast(I32))
 
-        nc.sync.dma_start(offs_sb[:], offs)
-
-        def load_words(name, words):
-            raw_w = new(name + "_raw_w", [P, 2 * W], U8)
+        def load_fp4_words(name, words):
+            raw_w = new(name, [P, 2 * W], U8)
             nc.sync.dma_start(raw_w[:].bitcast(I32), words[0].bitcast(I32))
             return raw_w
 
-        def load_scales(scales, raw_s):
-            for q in range(4):
-                nc.sync.dma_start(raw_s[32 * q : 32 * q + 4, :].bitcast(I32), scales[0, 4 * q : 4 * q + 4, :].bitcast(I32))
-            return raw_s
-
-        def load_factor(engine, rows, j, g):
-            engine.dma_start(
-                rows[4 * j : 4 * j + 4, :].rearrange("t (b r) -> t b r", r=8),
+        def load_factor(rows, first_row, g):
+            nc.sync.dma_start(
+                rows[first_row : first_row + 4, :].rearrange("t (b r) -> t b r", r=8),
                 g.rearrange("(b t r) o -> t b (r o)", t=4, r=8),
             )
 
         def turn(name, rows, n):
-            g_ps = bank(name + "_ps")
-            nc.tensor.transpose(g_ps[:, 0:P], rows[:], ident[:])
-            g_cols = new(name, [P, n], F32)
-            nc.scalar.copy(g_cols[:], g_ps[:, 0:n])
-            return g_cols
+            turned = bank(name + "_ps")
+            nc.tensor.transpose(turned[:, 0:P], rows[:], ident[:])
+            columns = new(name, [P, n], F32)
+            nc.scalar.copy(columns[:], turned[:, 0:n])
+            return columns
 
-        load_factor(nc.sync, g_rows[0], 0, gq)
+        nc.sync.dma_start(qs_sb[:], qs)
+        load_scales(xs, x_scales)
+        nc.sync.dma_start(offs_sb[:], offs)
+        load_factor(gq_rows, 0, gq)
         nc.sync.dma_start(xw[:], x_words[0].rearrange("p n t -> p (n t)").bitcast(I32))
-        w2_raw_w = load_words("w2", w2_words)
-        w2_raw = (w2_raw_w, load_scales(w2_scales, w_raw_s[0]))
-        load_factor(nc.sync, g_rows[1], 0, gk)
+        w2_raw_w = load_fp4_words("w2_raw_w", w2_words)
+        load_scales(w2_raw_s, w2_scales)
+        load_factor(gk_rows, 0, gk)
         ident = new("ident", [P, P], F32)
         make_identity(nc, ident[:])
-        gq_c = turn("gq_cols", g_rows[0], 4)[:, 0:4]
-        gk_c = turn("gk_cols", g_rows[1], 4)[:, 0:4]
-        w1_raw = (load_words("w1", w1_words), load_scales(w1_scales, w_raw_s[1]))
+        gq_c = turn("gq_cols", gq_rows, 4)[:, 0:4]
+        gk_c = turn("gk_cols", gk_rows, 4)[:, 0:4]
+        w1_raw_w = load_fp4_words("w1_raw_w", w1_words)
+        load_scales(w1_raw_s, w1_scales)
         nc.sync.dma_start(nb_sb[:], nb)
         wv_rows = wv.rearrange("(p j) c -> p j c", j=4)
         wv_raw = [new("wv_raw%d" % h, [P, 4, HALF], F32) for h in range(2)]
         for h in range(2):
-            nc.sync.dma_start(wv_raw[h][:], wv_rows[:, :, h * HALF : (h + 1) * HALF])
-        load_factor(nc.sync, g_rows[2], 0, gi)
-        load_factor(nc.sync, g_rows[2], 1, gt)
+            nc.sync.dma_start(wv_raw[h][:], wv_rows[:, :, cols(h * HALF, HALF)])
+        load_factor(token_rows, 0, gi)
+        load_factor(token_rows, 4, gt)
+        res_sb = new("res_sb", [P, 4, W], F32)
+        nc.sync.dma_start(res_sb[:], res.rearrange("(p t) v -> p t v", t=4))
 
         def deal(engine, name, raw, width, over=None):
             dealt = new(name, [P, width], U8, over)
@@ -110,47 +116,46 @@ def tile_picked_listsmooth_sigmoid_po_kernel(
             )
             return dealt
 
-        res_sb = new("res_sb", [P, 4, W], F32)
-        nc.sync.dma_start(res_sb[:], res.rearrange("(p t) v -> p t v", t=4))
-
         q_scale = new("q_scale", [P, W], U8)
         nc.vector.tensor_copy(q_scale[:], xs[:].indirect(qs_sb[:]))
         k_scale_raw = new("k_scale_raw", [P, W], U8)
         nc.vector.tensor_copy(k_scale_raw[:], xs[:].indirect(offs_sb[:]))
-        q_words = [new("q_words0", [P, HALF], U32)]
-        nc.vector.tensor_copy(q_words[0][:], xw[:].bitcast(U32).indirect(qs_sb[:, 0:16]))
-        w2_w = deal(nc.gpsimd, "w2_w", w2_raw[0], 2 * W)
-        w2_s = deal(nc.gpsimd, "w2_s", w2_raw[1], W)
-        q_words.append(new("q_words1", [P, HALF], U32))
-        nc.vector.tensor_copy(q_words[1][:], xw[:].bitcast(U32).indirect(qs_sb[:, 16:32]))
+        q_words0 = new("q_words0", [P, HALF], U32)
+        nc.vector.tensor_copy(q_words0[:], xw[:].bitcast(U32).indirect(entries(qs_sb, 0, HALF)))
+        w2_w = deal(nc.gpsimd, "w2_w", w2_raw_w, 2 * W)
+        w2_s = deal(nc.gpsimd, "w2_s", w2_raw_s, W)
+        q_words1 = new("q_words1", [P, HALF], U32)
+        nc.vector.tensor_copy(q_words1[:], xw[:].bitcast(U32).indirect(entries(qs_sb, HALF, HALF)))
         k_words = new("k_words", [P, W], U32)
         nc.vector.tensor_copy(
             k_words[:].rearrange("p (t b r) -> p b t r", t=4, b=16), xw[:].bitcast(U32).indirect(offs_sb[:])
         )
-        k_scale = deal(nc.vector, "k_scale", k_scale_raw, W, "w2_raw_w")
-        w1_w = deal(nc.gpsimd, "w1_w", w1_raw[0], 2 * W)
-        w1_s = deal(nc.gpsimd, "w1_s", w1_raw[1], W)
+        k_scale = deal(nc.vector, "k_scale", k_scale_raw, W, over="w2_raw_w")
+        w1_w = deal(nc.gpsimd, "w1_w", w1_raw_w, 2 * W)
+        w1_s = deal(nc.gpsimd, "w1_s", w1_raw_s, W)
 
         def mx(out, lhs, lhs_s, rhs, rhs_s):
             nc.tensor.matmul_mx(out=out, lhsT=lhs, lhsT_scale=lhs_s, rhs=rhs, rhs_scale=rhs_s, start=True, stop=True)
 
-        def fp4_slot(words, t):
-            return words[:, 2 * P * t : 2 * P * (t + 1)].bitcast(FP4X4)
+        def w2_slot(t):
+            return w2_w[:, cols(2 * P * t, 2 * P)].bitcast(FP4X4), w2_s[:, cols(t * P, P)]
 
-        def cols(c0, n):
-            return slice(c0, c0 + n)
+        def w1_slot(t):
+            return w1_w[:, cols(2 * P * t, 2 * P)].bitcast(FP4X4), w1_s[:, cols(t * P, P)]
+
+        def k_slot(t):
+            return k_words[:, cols(t * P, P)].bitcast(FP8X4), k_scale[:, cols(t * P, P)]
 
         def weave(engine_copy, woven, planes):
             engine_copy(
                 woven.rearrange("p (c i t) -> p c t i", i=4, t=4), planes.rearrange("p t (c i) -> p c t i", i=4)
             )
-            return woven
 
-        def quantise(codes, scales, woven):
-            nc.vector.quantize_mx(out=codes.bitcast(FP8X4), scales=scales, in_=woven)
+        def quantise(codes, scales, woven, c0, n):
+            nc.vector.quantize_mx(out=codes[:, cols(c0, n)].bitcast(FP8X4), scales=scales[:, cols(c0, n)], in_=woven)
 
-        def scaled_planes(name, lhs_slot, rhs, rhs_s, n, g, over=None):
-            planes = new(name + "_planes", [P, 4, n], BF16, over)
+        def planes_by_scalar(name, lhs_slot, rhs, rhs_s, n, g):
+            planes = new(name + "_planes", [P, 4, n], BF16)
             per_bank = W // n
             for t0 in range(0, 4, per_bank):
                 acc = bank(name + "_acc%d" % t0)
@@ -160,7 +165,7 @@ def tile_picked_listsmooth_sigmoid_po_kernel(
                     nc.scalar.activation(planes[:, t, :], acc[:, cols((t - t0) * n, n)], ACT.Copy, scale=g[:, t : t + 1])
             return planes[:]
 
-        def by_vector(name, woven, lhs_slot, rhs, rhs_s, g):
+        def woven_by_vector(name, woven, lhs_slot, rhs, rhs_s, g):
             acc = bank(name + "_acc")
             for t in range(4):
                 mx(acc[:, cols(t * P, P)], *lhs_slot(t), rhs, rhs_s)
@@ -170,38 +175,37 @@ def tile_picked_listsmooth_sigmoid_po_kernel(
                 g.unsqueeze(1).to_broadcast([P, P, 4]),
                 ALU.mult,
             )
-            return woven
-
-        def w2_slot(t):
-            return fp4_slot(w2_w, t), w2_s[:, cols(t * P, P)]
-
-        def w1_slot(t):
-            return fp4_slot(w1_w, t), w1_s[:, cols(t * P, P)]
-
-        def k_slot(t):
-            return k_words[:, cols(t * P, P)].bitcast(FP8X4), k_scale[:, cols(t * P, P)]
 
         z2_c = new("z2_c", [P, W], U32)
         z2_s = new("z2_s", [P, W], U8)
         z_c = new("z_c", [P, W], U32)
         z_s = new("z_s", [P, W], U8)
         z2_woven = new("z2_woven", [P, 4 * W], BF16)
-        planes0 = scaled_planes("z2_0", w2_slot, q_words[0][:].bitcast(FP8X4), q_scale[:, 0:HALF], HALF, gq_c)
-        planes2 = scaled_planes("z2_2", w2_slot, q_words[1][:, 0:P].bitcast(FP8X4), q_scale[:, cols(HALF, P)], P, gq_c)
-        by_vector("z2_3", z2_woven[:, cols(4 * P * 3, 4 * P)], w2_slot, q_words[1][:, cols(P, P)].bitcast(FP8X4), q_scale[:, cols(3 * P, P)], gq_c)
-        weave(nc.vector.tensor_copy, z2_woven[:, 0 : 4 * HALF], planes0)
-        weave(nc.vector.tensor_copy, z2_woven[:, cols(4 * HALF, 4 * P)], planes2)
-        quantise(z2_c[:], z2_s[:], z2_woven[:])
+        first_half = planes_by_scalar("z2_0", w2_slot, q_words0[:].bitcast(FP8X4), q_scale[:, 0:HALF], HALF, gq_c)
+        third_quarter = planes_by_scalar("z2_2", w2_slot, q_words1[:, 0:P].bitcast(FP8X4), q_scale[:, cols(2 * P, P)], P, gq_c)
+        woven_by_vector(
+            "z2_3", z2_woven[:, cols(4 * 3 * P, 4 * P)], w2_slot, q_words1[:, cols(P, P)].bitcast(FP8X4), q_scale[:, cols(3 * P, P)], gq_c
+        )
+        weave(nc.vector.tensor_copy, z2_woven[:, 0 : 4 * HALF], first_half)
+        weave(nc.vector.tensor_copy, z2_woven[:, cols(4 * 2 * P, 4 * P)], third_quarter)
         for c0 in (0, HALF):
-            planes = scaled_planes("z_%d" % c0, w1_slot, k_words[:, cols(c0, HALF)].bitcast(FP8X4), k_scale[:, cols(c0, HALF)], HALF, gk_c)
+            quantise(z2_c, z2_s, z2_woven[:, cols(4 * c0, 4 * HALF)], c0, HALF)
+
+        for c0 in (0, HALF):
+            planes = planes_by_scalar(
+                "z_%d" % c0, w1_slot, k_words[:, cols(c0, HALF)].bitcast(FP8X4), k_scale[:, cols(c0, HALF)], HALF, gk_c
+            )
             woven = new("z_woven%d" % c0, [P, 4 * HALF], BF16)
-            weave(nc.vector.tensor_copy, woven[:], planes)
-            quantise(z_c[:, cols(c0, HALF)], z_s[:, cols(c0, HALF)], woven[:])
+            for j in (0, P):
+                weave(nc.vector.tensor_copy, woven[:, cols(4 * j, 4 * P)], planes[:, :, cols(j, P)])
+            for j in (0, P):
+                quantise(z_c, z_s, woven[:, cols(4 * j, 4 * P)], c0 + j, P)
+
         wv_woven = new("wv_woven", [P, 4 * W], BF16)
 
         def weave_wv(engine_copy, h):
             engine_copy(
-                wv_woven[:].rearrange("p (t m j) -> p m j t", t=4, j=4)[:, 64 * h : 64 * h + 64],
+                wv_woven[:].rearrange("p (t m j) -> p m j t", t=4, j=4)[:, cols(64 * h, 64)],
                 wv_raw[h][:].rearrange("p j (m t) -> p m j t", t=4),
             )
 
@@ -219,14 +223,14 @@ def tile_picked_listsmooth_sigmoid_po_kernel(
             else:
                 nc.sync.dma_start(plains[t], windows[t][:, 0:W])
 
-        g_cols = turn("g_cols", g_rows[2], 8)
-        gi_c, gt_c = g_cols[:, 0:4], g_cols[:, 4:8]
+        token_cols = turn("g_cols", token_rows, 8)
+        gi_c, gt_c = token_cols[:, 0:4], token_cols[:, 4:8]
         weave_wv(nc.vector.tensor_copy, 1)
         wv_c = new("wv_c", [P, W], U32)
         wv_s = new("wv_s", [P, W], U8)
-        quantise(wv_c[:], wv_s[:], wv_woven[:])
+        quantise(wv_c, wv_s, wv_woven[:], 0, W)
         zv_s = new("zv_s", [P, W], U8)
-        zv_planes = scaled_planes("zv", k_slot, wv_c[:, 0:HALF].bitcast(FP8X4), wv_s[:, 0:HALF], HALF, gi_c)
+        zv_planes = planes_by_scalar("zv", k_slot, wv_c[:, 0:HALF].bitcast(FP8X4), wv_s[:, 0:HALF], HALF, gi_c)
 
         sums = new("sums", [P, 4, W], F32)
         sig = new("sig", [P, 4, W], F32)
@@ -234,7 +238,7 @@ def tile_picked_listsmooth_sigmoid_po_kernel(
 
         def smooth(t, c0, n):
             nc.vector.tensor_tensor(
-                sums[:, t, cols(c0, n)], windows[t][:].indirect(nb_sb[:, c0 // 16 : (c0 + n) // 16]), plains[t][:, cols(c0, n)], ALU.add
+                sums[:, t, cols(c0, n)], windows[t][:].indirect(entries(nb_sb, c0, n)), plains[t][:, cols(c0, n)], ALU.add
             )
 
         def gate(t, c0, n):
@@ -246,59 +250,64 @@ def tile_picked_listsmooth_sigmoid_po_kernel(
                 scale=gt_c[:, t : t + 1],
             )
 
-        smooth(0, 0, HALF)
-        smooth(0, HALF, HALF)
+        for c0 in (0, HALF):
+            smooth(0, c0, HALF)
         gate(0, 0, W)
         smooth(1, 0, W)
         gate(1, 0, W)
         zv_woven = new("zv_woven", [P, 4 * W], BF16)
         for c in (2, 3):
-            by_vector("zv_%d" % c, zv_woven[:, cols(4 * P * c, 4 * P)], k_slot, wv_c[:, cols(c * P, P)].bitcast(FP8X4), wv_s[:, cols(c * P, P)], gi_c)
+            woven_by_vector(
+                "zv_%d" % c, zv_woven[:, cols(4 * P * c, 4 * P)], k_slot, wv_c[:, cols(c * P, P)].bitcast(FP8X4), wv_s[:, cols(c * P, P)], gi_c
+            )
         weave(nc.vector.tensor_copy, zv_woven[:, 0 : 4 * HALF], zv_planes)
         smooth(2, 0, W)
         gate(2, 0, W)
-        for h in range(2):
-            smooth(3, h * HALF, HALF)
-            gate(3, h * HALF, HALF)
+        for c0 in (0, HALF):
+            smooth(3, c0, HALF)
+            gate(3, c0, HALF)
 
         zv_c = new("zv_c", [P, W], U32, over="s_plain3")
-        quantise(zv_c[:], zv_s[:], zv_woven[:])
+        quantise(zv_c, zv_s, zv_woven[:], 0, W)
+
         zp_woven = [new("zp_woven%d" % h, [P, 4 * HALF], BF16) for h in range(2)]
-        weave(nc.vector.tensor_copy, zp_woven[0][:], zp_planes[:, 0])
-        weave(nc.scalar.copy, zp_woven[1][:, 0 : 4 * P], zp_planes[:, 1, :, 0:P])
-        zp = []
+        zp_c = new("zp_c", [P, W], U32)
+        zp_s = new("zp_s", [P, W], U8)
         for h in range(2):
-            if h == 1:
-                weave(nc.vector.tensor_copy, zp_woven[1][:, 4 * P :], zp_planes[:, 1, :, P:])
-            zp_c = new("zp_c%d" % h, [P, HALF], U32)
-            zp_s = new("zp_s%d" % h, [P, HALF], U8)
-            quantise(zp_c[:], zp_s[:], zp_woven[h][:])
-            zp.extend((zp_c, zp_s, cols(j, P)) for j in (0, P))
+            for j in (0, P):
+                engine_copy = nc.scalar.copy if (h, j) == (1, 0) else nc.vector.tensor_copy
+                weave(engine_copy, zp_woven[h][:, cols(4 * j, 4 * P)], zp_planes[:, h, :, cols(j, P)])
+            for j in (0, P):
+                quantise(zp_c, zp_s, zp_woven[h][:, cols(4 * j, 4 * P)], h * HALF + j, P)
 
         y_s = new("y_s", [P, W], U8)
         out_rows = out_0.rearrange("(p t) v -> p t v", t=4)
         out_words = out_1[0].rearrange("p n t -> p (n t)").bitcast(I32)
-        y_half = [new("y_woven%d" % h, [P, 4 * HALF], BF16) for h in range(2)]
+        y_woven = [new("y_woven%d" % h, [P, 4 * HALF], BF16) for h in range(2)]
         for c in range(4):
-            zp_c, zp_s, part = zp[c]
+            quarter = cols(c * P, P)
             acc = bank("out_acc%d" % c)
             for t in range(4):
                 mx(
                     acc[:, cols(t * P, P)],
                     zv_c[:, cols(t * P, P)].bitcast(FP8X4),
                     zv_s[:, cols(t * P, P)],
-                    zp_c[:, part].bitcast(FP8X4),
-                    zp_s[:, part],
+                    zp_c[:, quarter].bitcast(FP8X4),
+                    zp_s[:, quarter],
                 )
-            y = new("y%d" % c, [P, 4, P], F32, "zp_woven1" if c == 0 else None)
+            y = new("y%d" % c, [P, 4, P], F32, over="zp_woven1" if c == 1 else None)
             nc.vector.scalar_tensor_tensor(
-                y[:], acc[:].rearrange("p (t n) -> p t n", t=4), SIXTEENTH, res_sb[:, :, cols(c * P, P)], ALU.mult, ALU.add
+                y[:], acc[:].rearrange("p (t n) -> p t n", t=4), SIXTEENTH, res_sb[:, :, quarter], ALU.mult, ALU.add
             )
-            nc.sync.dma_start(out_rows[:, :, cols(c * P, P)], y[:])
-            weave(nc.vector.tensor_copy if c == 3 else nc.scalar.copy, y_half[c // 2][:, cols((c % 2) * 4 * P, 4 * P)], y[:])
-        for h in range(2):
+            nc.sync.dma_start(out_rows[:, :, quarter], y[:])
+            weave(nc.vector.tensor_copy if c == 3 else nc.scalar.copy, y_woven[c // 2][:, cols((c % 2) * 4 * P, 4 * P)], y[:])
+
+        for h, pieces in enumerate((((0, HALF),), ((0, P), (P, P)))):
             y_c = new("y_c%d" % h, [P, HALF], U32)
-            quantise(y_c[:], y_s[:, cols(h * HALF, HALF)], y_half[h][:])
+            for j, n in pieces:
+                quantise(y_c, y_s[:, cols(h * HALF, HALF)], y_woven[h][:, cols(4 * j, 4 * n)], j, n)
             nc.sync.dma_start(out_words[:, cols(h * HALF, HALF)], y_c[:].bitcast(I32))
         for q in range(4):
-            (nc.scalar if q % 2 else nc.sync).dma_start(out_2[0, 4 * q : 4 * q + 4, :].bitcast(I32), y_s[32 * q : 32 * q + 4, :].bitcast(I32))
+            (nc.scalar if q % 2 else nc.sync).dma_start(
+                out_2[0, 4 * q : 4 * q + 4, :].bitcast(I32), y_s[32 * q : 32 * q + 4, :].bitcast(I32)
+            )

@@ -50,7 +50,7 @@ def tile_picked_listsmooth_sigmoid_po_kernel(
         nb_sb = lists.tile([P, W // ENTRIES], U16, name="nb_sb")
         xs = new("xs", [P, T], U8)
         xw = new("xw", [P, T], I32)
-        nc.gpsimd.memset(xs[:].bitcast(I32), 0)
+        nc.vector.memset(xs[:].bitcast(I32), 0)
         w2_raw_s, w1_raw_s = new("w2_raw_s", [P, W], U8), new("w1_raw_s", [P, W], U8)
         for raw_s in (w2_raw_s, w1_raw_s):
             nc.vector.memset(raw_s[:].bitcast(I32), 0)
@@ -85,18 +85,18 @@ def tile_picked_listsmooth_sigmoid_po_kernel(
             return columns
 
         nc.sync.dma_start(qs_sb[:], qs)
-        load_scales(xs, x_scales)
-        nc.sync.dma_start(offs_sb[:], offs)
-        load_factor(gq_rows, 0, gq)
-        nc.sync.dma_start(xw[:], x_words[0].rearrange("p n t -> p (n t)").bitcast(I32))
         w2_raw_w = load_fp4_words("w2_raw_w", w2_words)
+        nc.sync.dma_start(offs_sb[:], offs)
+        load_scales(xs, x_scales)
+        nc.sync.dma_start(xw[:], x_words[0].rearrange("p n t -> p (n t)").bitcast(I32))
+        load_factor(gq_rows, 0, gq)
         load_scales(w2_raw_s, w2_scales)
+        w1_raw_w = load_fp4_words("w1_raw_w", w1_words)
         load_factor(gk_rows, 0, gk)
         ident = new("ident", [P, P], F32)
         make_identity(nc, ident[:])
         gq_c = turn("gq_cols", gq_rows, 4)[:, 0:4]
         gk_c = turn("gk_cols", gk_rows, 4)[:, 0:4]
-        w1_raw_w = load_fp4_words("w1_raw_w", w1_words)
         load_scales(w1_raw_s, w1_scales)
         nc.sync.dma_start(nb_sb[:], nb)
         wv_rows = wv.rearrange("(p j) c -> p j c", j=4)
@@ -130,7 +130,7 @@ def tile_picked_listsmooth_sigmoid_po_kernel(
         nc.vector.tensor_copy(
             k_words[:].rearrange("p (t b r) -> p b t r", t=4, b=16), xw[:].bitcast(U32).indirect(offs_sb[:])
         )
-        k_scale = deal(nc.vector, "k_scale", k_scale_raw, W, over="w2_raw_w")
+        k_scale = deal(nc.vector, "k_scale", k_scale_raw, W, over="w2_raw_s")
         w1_w = deal(nc.gpsimd, "w1_w", w1_raw_w, 2 * W)
         w1_s = deal(nc.gpsimd, "w1_s", w1_raw_s, W)
 

@@ -241,8 +241,10 @@ def tile_picked_listsmooth_sigmoid_po_kernel(
                 sums[:, t, cols(c0, n)], windows[t][:].indirect(entries(nb_sb, c0, n)), plains[t][:, cols(c0, n)], ALU.add
             )
 
-        def gate(t, c0, n):
+        def squash(t, c0, n):
             nc.scalar.activation(sig[:, t, cols(c0, n)], sums[:, t, cols(c0, n)], ACT.Sigmoid)
+
+        def gate(t, c0, n):
             nc.scalar.activation(
                 zp_planes[:, c0 // HALF : (c0 + n) // HALF, t, :],
                 sig[:, t, cols(c0, n)].rearrange("p (h c) -> p h c", c=HALF),
@@ -252,9 +254,10 @@ def tile_picked_listsmooth_sigmoid_po_kernel(
 
         for c0 in (0, HALF):
             smooth(0, c0, HALF)
-        gate(0, 0, W)
         smooth(1, 0, W)
-        gate(1, 0, W)
+        for step in (squash, gate):
+            for t in (0, 1):
+                step(t, 0, W)
         zv_woven = new("zv_woven", [P, 4 * W], BF16)
         for c in (2, 3):
             woven_by_vector(
@@ -262,9 +265,13 @@ def tile_picked_listsmooth_sigmoid_po_kernel(
             )
         weave(nc.vector.tensor_copy, zv_woven[:, 0 : 4 * HALF], zv_planes)
         smooth(2, 0, W)
-        gate(2, 0, W)
         for c0 in (0, HALF):
             smooth(3, c0, HALF)
+        squash(2, 0, W)
+        squash(3, 0, HALF)
+        gate(2, 0, W)
+        squash(3, HALF, HALF)
+        for c0 in (0, HALF):
             gate(3, c0, HALF)
 
         zv_c = new("zv_c", [P, W], U32, over="s_plain3")

@@ -63,8 +63,8 @@ def tile_picked_listsmooth_sigmoid_po_kernel(
         nc.scalar.activation(warm[:], warm_in[:], ACT.Sigmoid)
 
         def load_scales(tile, scales):
-            for q in range(4):
-                nc.sync.dma_start(tile[32 * q : 32 * q + 4, :].bitcast(I32), scales[0, 4 * q : 4 * q + 4, :].bitcast(I32))
+            for r in range(4):
+                nc.sync.dma_start(tile[r:P:32, :].bitcast(I32), scales[0, r:16:4, :].bitcast(I32))
 
         def load_fp4_words(name, words):
             raw_w = new(name, [P, 2 * W], U8)
@@ -314,7 +314,5 @@ def tile_picked_listsmooth_sigmoid_po_kernel(
             for j, n in pieces:
                 quantise(y_c, y_s[:, cols(h * HALF, HALF)], y_woven[h][:, cols(4 * j, 4 * n)], j, n)
             nc.sync.dma_start(out_words[:, cols(h * HALF, HALF)], y_c[:].bitcast(I32))
-        for q in range(4):
-            (nc.scalar if q % 2 else nc.sync).dma_start(
-                out_2[0, 4 * q : 4 * q + 4, :].bitcast(I32), y_s[32 * q : 32 * q + 4, :].bitcast(I32)
-            )
+        for r in range(4):
+            (nc.scalar if r % 2 else nc.sync).dma_start(out_2[0, r:16:4, :].bitcast(I32), y_s[r:P:32, :].bitcast(I32))

@@ -191,25 +191,31 @@ def tile_picked_listsmooth_sigmoid_po_kernel(
         for c0 in (0, HALF):
             quantise(z2_c, z2_s, z2_woven[:, cols(4 * c0, 4 * HALF)], c0, HALF)
 
+        wv_woven = new("wv_woven", [P, 4 * W], BF16)
+
+        def weave_wv(engine_copy, h, m0, n):
+            engine_copy(
+                wv_woven[:].rearrange("p (t m j) -> p m j t", t=4, j=4)[:, cols(64 * h + m0, n)],
+                wv_raw[h][:].rearrange("p j (m t) -> p m j t", t=4)[:, cols(m0, n)],
+            )
+
         for c0 in (0, HALF):
             planes = planes_by_scalar(
                 "z_%d" % c0, w1_slot, k_words[:, cols(c0, HALF)].bitcast(FP8X4), k_scale[:, cols(c0, HALF)], HALF, gk_c
             )
             woven = new("z_woven%d" % c0, [P, 4 * HALF], BF16)
-            for j in (0, P):
-                weave(nc.vector.tensor_copy, woven[:, cols(4 * j, 4 * P)], planes[:, :, cols(j, P)])
-            for j in (0, P):
-                quantise(z_c, z_s, woven[:, cols(4 * j, 4 * P)], c0 + j, P)
+            if c0 == 0:
+                for j in (0, P):
+                    weave(nc.vector.tensor_copy, woven[:, cols(4 * j, 4 * P)], planes[:, :, cols(j, P)])
+                for j in (0, P):
+                    quantise(z_c, z_s, woven[:, cols(4 * j, 4 * P)], j, P)
+            else:
+                weave(nc.vector.tensor_copy, woven[:], planes)
+                weave_wv(nc.vector.tensor_copy, 1, 0, 64)
+                weave_wv(nc.vector.tensor_copy, 0, 40, 24)
+                quantise(z_c, z_s, woven[:], c0, HALF)
 
-        wv_woven = new("wv_woven", [P, 4 * W], BF16)
-
-        def weave_wv(engine_copy, h):
-            engine_copy(
-                wv_woven[:].rearrange("p (t m j) -> p m j t", t=4, j=4)[:, cols(64 * h, 64)],
-                wv_raw[h][:].rearrange("p j (m t) -> p m j t", t=4),
-            )
-
-        weave_wv(nc.scalar.copy, 0)
+        weave_wv(nc.scalar.copy, 0, 0, 40)
 
         windows = [new("s_window%d" % t, [P, 2 * W if t else W], F32) for t in range(4)]
         plain3 = new("s_plain3", [P, W], F32)
@@ -225,12 +231,13 @@ def tile_picked_listsmooth_sigmoid_po_kernel(
 
         token_cols = turn("g_cols", token_rows, 8)
         gi_c, gt_c = token_cols[:, 0:4], token_cols[:, 4:8]
-        weave_wv(nc.vector.tensor_copy, 1)
         wv_c = new("wv_c", [P, W], U32)
         wv_s = new("wv_s", [P, W], U8)
         quantise(wv_c, wv_s, wv_woven[:], 0, W)
         zv_s = new("zv_s", [P, W], U8)
-        zv_planes = planes_by_scalar("zv", k_slot, wv_c[:, 0:HALF].bitcast(FP8X4), wv_s[:, 0:HALF], HALF, gi_c)
+        zv_quarters = [
+            planes_by_scalar("zv%d" % c, k_slot, wv_c[:, cols(c * P, P)].bitcast(FP8X4), wv_s[:, cols(c * P, P)], P, gi_c) for c in range(2)
+        ]
 
         sums = new("sums", [P, 4, W], F32)
         sig = new("sig", [P, 4, W], F32)
@@ -263,7 +270,15 @@ def tile_picked_listsmooth_sigmoid_po_kernel(
             woven_by_vector(
                 "zv_%d" % c, zv_woven[:, cols(4 * P * c, 4 * P)], k_slot, wv_c[:, cols(c * P, P)].bitcast(FP8X4), wv_s[:, cols(c * P, P)], gi_c
             )
-        weave(nc.vector.tensor_copy, zv_woven[:, 0 : 4 * HALF], zv_planes)
+        nc.gpsimd.tensor_scalar(
+            zv_woven[:, 0 : 4 * P].rearrange("p (c t) -> p c t", t=4),
+            zv_quarters[0].rearrange("p t c -> p c t"),
+            1.0,
+            0.0,
+            ALU.mult,
+            ALU.add,
+        )
+        weave(nc.vector.tensor_copy, zv_woven[:, cols(4 * P, 4 * P)], zv_quarters[1])
         smooth(2, 0, W)
         for c0 in (0, HALF):
             smooth(3, c0, HALF)

@@ -306,6 +306,11 @@ def tile_picked_listsmooth_sigmoid_po_kernel(
         out_rows = out_0.rearrange("(p t) v -> p t v", t=4)
         out_words = out_1[0].rearrange("p n t -> p (n t)").bitcast(I32)
         y_woven = [new("y_woven%d" % h, [P, 4 * HALF], BF16) for h in range(2)]
+        y_first = new("y_first", [P, 4, P], F32)
+        y_middle = new("y_middle", [P, 4, HALF], F32, over="zp_woven1")
+        y_last = new("y_last", [P, 4, P], F32)
+        ys = (y_first[:], y_middle[:, :, 0:P], y_middle[:, :, P:], y_last[:])
+        stores = {0: (y_first, 0, P), 2: (y_middle, P, HALF), 3: (y_last, 3 * P, P)}
         for c in range(4):
             quarter = cols(c * P, P)
             acc = bank("out_acc%d" % c)
@@ -317,17 +322,18 @@ def tile_picked_listsmooth_sigmoid_po_kernel(
                     zp_c[:, quarter].bitcast(FP8X4),
                     zp_s[:, quarter],
                 )
-            y = new("y%d" % c, [P, 4, P], F32, over="zp_woven1" if c == 1 else None)
             nc.vector.scalar_tensor_tensor(
-                y[:], acc[:].rearrange("p (t n) -> p t n", t=4), SIXTEENTH, res_sb[:, :, quarter], ALU.mult, ALU.add
+                ys[c], acc[:].rearrange("p (t n) -> p t n", t=4), SIXTEENTH, res_sb[:, :, quarter], ALU.mult, ALU.add
             )
-            nc.sync.dma_start(out_rows[:, :, quarter], y[:])
-            weave(nc.vector.tensor_copy if c == 3 else nc.scalar.copy, y_woven[c // 2][:, cols((c % 2) * 4 * P, 4 * P)], y[:])
+            if c in stores:
+                y, c0, n = stores[c]
+                nc.sync.dma_start(out_rows[:, :, cols(c0, n)], y[:])
+            weave(nc.vector.tensor_copy if c == 3 else nc.scalar.copy, y_woven[c // 2][:, cols((c % 2) * 4 * P, 4 * P)], ys[c])
 
-        for h, pieces in enumerate((((0, HALF),), ((0, P), (P, P)))):
-            y_c = new("y_c%d" % h, [P, HALF], U32)
-            for j, n in pieces:
-                quantise(y_c, y_s[:, cols(h * HALF, HALF)], y_woven[h][:, cols(4 * j, 4 * n)], j, n)
-            nc.sync.dma_start(out_words[:, cols(h * HALF, HALF)], y_c[:].bitcast(I32))
+        y_c = new("y_c", [P, W], U32)
+        quantise(y_c, y_s, y_woven[0][:], 0, HALF)
+        for j in (0, P):
+            quantise(y_c, y_s, y_woven[1][:, cols(4 * j, 4 * P)], HALF + j, P)
+        nc.sync.dma_start(out_words, y_c[:].bitcast(I32))
         for r in range(4):
             (nc.scalar if r % 2 else nc.sync).dma_start(out_2[0, r:16:4, :].bitcast(I32), y_s[r:P:32, :].bitcast(I32))

@@ -212,22 +212,18 @@ def tile_picked_listsmooth_sigmoid_po_kernel(
             else:
                 weave(nc.vector.tensor_copy, woven[:], planes)
                 weave_wv(nc.vector.tensor_copy, 1, 0, 64)
-                weave_wv(nc.vector.tensor_copy, 0, 40, 24)
                 quantise(z_c, z_s, woven[:], c0, HALF)
 
-        weave_wv(nc.scalar.copy, 0, 0, 40)
+        weave_wv(nc.scalar.copy, 0, 0, 64)
 
-        windows = [new("s_window%d" % t, [P, 2 * W if t else W], F32) for t in range(4)]
-        plain3 = new("s_plain3", [P, W], F32)
-        plains = [windows[t + 1][:, W:] for t in range(3)] + [plain3[:]]
+        windows = [new("s_window%d" % t, [P, W], F32) for t in range(4)]
+        plains = {t: new("s_plain%d" % t, [P, W], F32) for t in (2, 3)}
         for t in range(4):
             acc = bank("s_acc%d" % t)
             mx(acc[:], z_c[:, cols(t * P, P)].bitcast(FP8X4), z_s[:, cols(t * P, P)], z2_c[:].bitcast(FP8X4), z2_s[:])
             nc.scalar.activation(windows[t][:, 0:W], acc[:], ACT.Copy, scale=SIXTEENTH)
-            if t < 2:
-                nc.scalar.activation(plains[t], acc[:], ACT.Copy, scale=SIXTEENTH)
-            else:
-                nc.sync.dma_start(plains[t], windows[t][:, 0:W])
+            if t in plains:
+                nc.sync.dma_start(plains[t][:], windows[t][:, 0:W])
 
         token_cols = turn("g_cols", token_rows, 8)
         gi_c, gt_c = token_cols[:, 0:4], token_cols[:, 4:8]
@@ -235,9 +231,6 @@ def tile_picked_listsmooth_sigmoid_po_kernel(
         wv_s = new("wv_s", [P, W], U8)
         quantise(wv_c, wv_s, wv_woven[:], 0, W)
         zv_s = new("zv_s", [P, W], U8)
-        zv_quarters = [
-            planes_by_scalar("zv%d" % c, k_slot, wv_c[:, cols(c * P, P)].bitcast(FP8X4), wv_s[:, cols(c * P, P)], P, gi_c) for c in range(2)
-        ]
 
         sums = new("sums", [P, 4, W], F32)
         sig = new("sig", [P, 4, W], F32)
@@ -259,35 +252,34 @@ def tile_picked_listsmooth_sigmoid_po_kernel(
                 scale=gt_c[:, t : t + 1],
             )
 
+        fetched0 = new("fetched0", [P, W], F32, over="z_c")
+        fetched1 = new("fetched1", [P, W], F32)
+        fetched = {1: fetched0[:], 0: fetched1[:]}
         for c0 in (0, HALF):
-            smooth(0, c0, HALF)
-        smooth(1, 0, W)
-        for step in (squash, gate):
-            for t in (0, 1):
-                step(t, 0, W)
+            nc.vector.tensor_copy(fetched[0][:, cols(c0, HALF)], windows[0][:].indirect(entries(nb_sb, c0, HALF)))
+            nc.scalar.activation(fetched[1][:, cols(c0, HALF)], windows[1][:].indirect(entries(nb_sb, c0, HALF)), ACT.Copy)
+        for t in (0, 1):
+            for c0 in (0, HALF):
+                nc.gpsimd.tensor_tensor(
+                    sums[:, t, cols(c0, HALF)], windows[t][:, cols(c0, HALF)], fetched[t][:, cols(c0, HALF)], ALU.add
+                )
+        squash(0, 0, W)
+        squash(1, 0, HALF)
+        gate(0, 0, W)
+        squash(1, HALF, HALF)
+        for c0 in (0, HALF):
+            gate(1, c0, HALF)
         zv_woven = new("zv_woven", [P, 4 * W], BF16)
-        for c in (2, 3):
+        for c in range(4):
             woven_by_vector(
                 "zv_%d" % c, zv_woven[:, cols(4 * P * c, 4 * P)], k_slot, wv_c[:, cols(c * P, P)].bitcast(FP8X4), wv_s[:, cols(c * P, P)], gi_c
             )
-        nc.gpsimd.tensor_scalar(
-            zv_woven[:, 0 : 4 * P].rearrange("p (c t) -> p c t", t=4),
-            zv_quarters[0].rearrange("p t c -> p c t"),
-            1.0,
-            0.0,
-            ALU.mult,
-            ALU.add,
-        )
-        weave(nc.vector.tensor_copy, zv_woven[:, cols(4 * P, 4 * P)], zv_quarters[1])
-        smooth(2, 0, W)
         for c0 in (0, HALF):
-            smooth(3, c0, HALF)
-        squash(2, 0, W)
-        squash(3, 0, HALF)
-        gate(2, 0, W)
-        squash(3, HALF, HALF)
-        for c0 in (0, HALF):
-            gate(3, c0, HALF)
+            for t in (2, 3):
+                smooth(t, c0, HALF)
+            for step in (squash, gate):
+                for t in (2, 3):
+                    step(t, c0, HALF)
 
         zv_c = new("zv_c", [P, W], U32, over="s_plain3")
         quantise(zv_c, zv_s, zv_woven[:], 0, W)

@@ -222,8 +222,10 @@ def tile_picked_listsmooth_sigmoid_po_kernel(
             acc = bank("s_acc%d" % t)
             mx(acc[:], z_c[:, cols(t * P, P)].bitcast(FP8X4), z_s[:, cols(t * P, P)], z2_c[:].bitcast(FP8X4), z2_s[:])
             nc.scalar.activation(windows[t][:, 0:W], acc[:], ACT.Copy, scale=SIXTEENTH)
-            if t in plains:
-                nc.sync.dma_start(plains[t][:], windows[t][:, 0:W])
+            if t == 2:
+                nc.sync.dma_start(plains[t][:, HALF:], windows[t][:, HALF:])
+            if t == 3:
+                nc.sync.dma_start(plains[t][:], windows[t][:])
 
         token_cols = turn("g_cols", token_rows, 8)
         gi_c, gt_c = token_cols[:, 0:4], token_cols[:, 4:8]
@@ -252,34 +254,36 @@ def tile_picked_listsmooth_sigmoid_po_kernel(
                 scale=gt_c[:, t : t + 1],
             )
 
-        fetched0 = new("fetched0", [P, W], F32, over="z_c")
-        fetched1 = new("fetched1", [P, W], F32)
-        fetched = {1: fetched0[:], 0: fetched1[:]}
-        for c0 in (0, HALF):
-            nc.vector.tensor_copy(fetched[0][:, cols(c0, HALF)], windows[0][:].indirect(entries(nb_sb, c0, HALF)))
-            nc.scalar.activation(fetched[1][:, cols(c0, HALF)], windows[1][:].indirect(entries(nb_sb, c0, HALF)), ACT.Copy)
-        for t in (0, 1):
-            for c0 in (0, HALF):
-                nc.gpsimd.tensor_tensor(
-                    sums[:, t, cols(c0, HALF)], windows[t][:, cols(c0, HALF)], fetched[t][:, cols(c0, HALF)], ALU.add
-                )
-        squash(0, 0, W)
+        first = new("fetched_first", [P, HALF], F32)
+        by_vector = new("fetched_by_vector", [P, 3, HALF], F32)
+        last = new("fetched_last", [P, HALF], F32, over="z_c")
+        pieces = [(0, 0, first[:]), (1, 0, by_vector[:, 0, :]), (0, HALF, by_vector[:, 1, :]), (2, 0, by_vector[:, 2, :]), (1, HALF, last[:])]
+        for n, (t, c0, fetched) in enumerate(pieces):
+            looked_up = windows[t][:].indirect(entries(nb_sb, c0, HALF))
+            if n in (1, 2, 3):
+                nc.vector.tensor_copy(fetched, looked_up)
+            else:
+                nc.scalar.activation(fetched, looked_up, ACT.Copy)
+            nc.gpsimd.tensor_tensor(sums[:, t, cols(c0, HALF)], windows[t][:, cols(c0, HALF)], fetched, ALU.add)
         squash(1, 0, HALF)
+        squash(0, 0, W)
+        gate(1, 0, HALF)
+        squash(2, 0, HALF)
         gate(0, 0, W)
         squash(1, HALF, HALF)
-        for c0 in (0, HALF):
-            gate(1, c0, HALF)
+        gate(2, 0, HALF)
         zv_woven = new("zv_woven", [P, 4 * W], BF16)
         for c in range(4):
             woven_by_vector(
                 "zv_%d" % c, zv_woven[:, cols(4 * P * c, 4 * P)], k_slot, wv_c[:, cols(c * P, P)].bitcast(FP8X4), wv_s[:, cols(c * P, P)], gi_c
             )
-        for c0 in (0, HALF):
+        smooth(3, 0, HALF)
+        squash(3, 0, HALF)
+        gate(1, HALF, HALF)
+        gate(3, 0, HALF)
+        for step in (smooth, squash, gate):
             for t in (2, 3):
-                smooth(t, c0, HALF)
-            for step in (squash, gate):
-                for t in (2, 3):
-                    step(t, c0, HALF)
+                step(t, HALF, HALF)
 
         zv_c = new("zv_c", [P, W], U32, over="s_plain3")
         quantise(zv_c, zv_s, zv_woven[:], 0, W)

@@ -31,7 +31,8 @@ def tile_picked_listsmooth_sigmoid_po_kernel(
     with ExitStack() as ctx:
         lists = ctx.enter_context(tc.tile_pool(name="lists", bufs=1))
         sb = ctx.enter_context(tc.tile_pool(name="sb", bufs=1))
-        psum = ctx.enter_context(tc.psum_pool(name="psum", bufs=8))
+        psum = ctx.enter_context(tc.psum_pool(name="psum", bufs=7))
+        held = ctx.enter_context(tc.psum_pool(name="held", bufs=1))
 
         def new(name, shape, dtype, over=None):
             return sb.tile(shape, dtype, name=name, tag=over or name, align_bytes=64)
@@ -54,8 +55,8 @@ def tile_picked_listsmooth_sigmoid_po_kernel(
         w2_raw_s, w1_raw_s = new("w2_raw_s", [P, W], U8), new("w1_raw_s", [P, W], U8)
         for raw_s in (w2_raw_s, w1_raw_s):
             nc.vector.memset(raw_s[:].bitcast(I32), 0)
-        gq_rows, gk_rows, token_rows = [new("g_rows%d" % j, [P, P], F32) for j in range(3)]
-        for rows in (gq_rows, gk_rows, token_rows):
+        feature_rows, token_rows = new("feature_rows", [P, P], F32), new("token_rows", [P, P], F32)
+        for rows in (feature_rows, token_rows):
             nc.vector.memset(rows[:], 0.0)
         warm_in = new("warm_in", [P, 1], F32)
         nc.vector.memset(warm_in[:], 0.0)
@@ -77,62 +78,64 @@ def tile_picked_listsmooth_sigmoid_po_kernel(
                 g.rearrange("(b t r) o -> t b (r o)", t=4, r=8),
             )
 
-        def turn(name, rows, n):
-            turned = bank(name + "_ps")
-            nc.tensor.transpose(turned[:, 0:P], rows[:], ident[:])
-            columns = new(name, [P, n], F32)
-            nc.scalar.copy(columns[:], turned[:, 0:n])
-            return columns
-
         nc.sync.dma_start(qs_sb[:], qs)
         w2_raw_w = load_fp4_words("w2_raw_w", w2_words)
         nc.sync.dma_start(offs_sb[:], offs)
         load_scales(xs, x_scales)
         nc.sync.dma_start(xw[:], x_words[0].rearrange("p n t -> p (n t)").bitcast(I32))
-        load_factor(gq_rows, 0, gq)
+        load_factor(feature_rows, 0, gq)
+        load_factor(feature_rows, 4, gk)
         load_scales(w2_raw_s, w2_scales)
         w1_raw_w = load_fp4_words("w1_raw_w", w1_words)
-        load_factor(gk_rows, 0, gk)
-        ident = new("ident", [P, P], F32)
-        make_identity(nc, ident[:])
-        gq_c = turn("gq_cols", gq_rows, 4)[:, 0:4]
-        gk_c = turn("gk_cols", gk_rows, 4)[:, 0:4]
-        load_scales(w1_raw_s, w1_scales)
-        nc.sync.dma_start(nb_sb[:], nb)
         wv_rows = wv.rearrange("(p j) c -> p j c", j=4)
-        wv_raw = [new("wv_raw%d" % h, [P, 4, HALF], F32) for h in range(2)]
-        for h in range(2):
-            nc.sync.dma_start(wv_raw[h][:], wv_rows[:, :, cols(h * HALF, HALF)])
+        wv_cuts = (0, HALF, 3 * P, W)
+        wv_raw = [new("wv_raw%d" % j, [P, 4, wv_cuts[j + 1] - wv_cuts[j]], F32) for j in range(3)]
+        load_scales(w1_raw_s, w1_scales)
+        for j in range(3):
+            nc.sync.dma_start(wv_raw[j][:], wv_rows[:, :, wv_cuts[j] : wv_cuts[j + 1]])
+        nc.sync.dma_start(nb_sb[:], nb)
         load_factor(token_rows, 0, gi)
         load_factor(token_rows, 4, gt)
         res_sb = new("res_sb", [P, 4, W], F32)
         nc.sync.dma_start(res_sb[:], res.rearrange("(p t) v -> p t v", t=4))
 
-        def deal(engine, name, raw, width, over=None):
-            dealt = new(name, [P, width], U8, over)
-            engine.tensor_copy(
+        ident = new("ident", [P, P], F32)
+        make_identity(nc, ident[:])
+        features_turned = bank("features_turned")
+        nc.tensor.transpose(features_turned[:, 0:P], feature_rows[:], ident[:])
+        feature_cols = new("feature_cols", [P, 8], F32)
+        nc.scalar.copy(feature_cols[:], features_turned[:, 0:8])
+        tokens_turned = held.tile([P, P], F32, name="tokens_turned")
+        nc.tensor.transpose(tokens_turned[:], token_rows[:], ident[:])
+        gi_cols = new("gi_cols", [P, 4], F32)
+        nc.scalar.copy(gi_cols[:], tokens_turned[:, 0:4])
+        gq_c, gk_c, gi_c, gt_c = feature_cols[:, 0:4], feature_cols[:, 4:8], gi_cols[:], tokens_turned[:, 4:8]
+
+        def deal(name, raw, width):
+            dealt = new(name, [P, width], U8)
+            nc.gpsimd.tensor_copy(
                 dealt[:].bitcast(I32).rearrange("p (t b u) -> p t b u", t=4, b=16),
                 raw[:].bitcast(I32).rearrange("p (b t u) -> p t b u", t=4, b=16),
             )
             return dealt
 
+        def dealt_by_slot(tile):
+            return tile[:].rearrange("p (t b r) -> p b t r", t=4, b=16)
+
         q_scale = new("q_scale", [P, W], U8)
         nc.vector.tensor_copy(q_scale[:], xs[:].indirect(qs_sb[:]))
-        k_scale_raw = new("k_scale_raw", [P, W], U8)
-        nc.vector.tensor_copy(k_scale_raw[:], xs[:].indirect(offs_sb[:]))
+        k_scale = new("k_scale", [P, W], U8)
+        nc.vector.tensor_copy(dealt_by_slot(k_scale), xs[:].indirect(offs_sb[:]))
         q_words0 = new("q_words0", [P, HALF], U32)
         nc.vector.tensor_copy(q_words0[:], xw[:].bitcast(U32).indirect(entries(qs_sb, 0, HALF)))
-        w2_w = deal(nc.gpsimd, "w2_w", w2_raw_w, 2 * W)
-        w2_s = deal(nc.gpsimd, "w2_s", w2_raw_s, W)
+        w2_w = deal("w2_w", w2_raw_w, 2 * W)
+        w2_s = deal("w2_s", w2_raw_s, W)
         q_words1 = new("q_words1", [P, HALF], U32)
         nc.vector.tensor_copy(q_words1[:], xw[:].bitcast(U32).indirect(entries(qs_sb, HALF, HALF)))
         k_words = new("k_words", [P, W], U32)
-        nc.vector.tensor_copy(
-            k_words[:].rearrange("p (t b r) -> p b t r", t=4, b=16), xw[:].bitcast(U32).indirect(offs_sb[:])
-        )
-        k_scale = deal(nc.vector, "k_scale", k_scale_raw, W, over="w2_raw_s")
-        w1_w = deal(nc.gpsimd, "w1_w", w1_raw_w, 2 * W)
-        w1_s = deal(nc.gpsimd, "w1_s", w1_raw_s, W)
+        nc.vector.tensor_copy(dealt_by_slot(k_words), xw[:].bitcast(U32).indirect(offs_sb[:]))
+        w1_w = deal("w1_w", w1_raw_w, 2 * W)
+        w1_s = deal("w1_s", w1_raw_s, W)
 
         def mx(out, lhs, lhs_s, rhs, rhs_s):
             nc.tensor.matmul_mx(out=out, lhsT=lhs, lhsT_scale=lhs_s, rhs=rhs, rhs_scale=rhs_s, start=True, stop=True)
@@ -146,10 +149,14 @@ def tile_picked_listsmooth_sigmoid_po_kernel(
         def k_slot(t):
             return k_words[:, cols(t * P, P)].bitcast(FP8X4), k_scale[:, cols(t * P, P)]
 
+        def as_woven(woven):
+            return woven.rearrange("p (c i t) -> p c t i", i=4, t=4)
+
+        def as_planes(planes):
+            return planes.rearrange("p t (c i) -> p c t i", i=4)
+
         def weave(engine_copy, woven, planes):
-            engine_copy(
-                woven.rearrange("p (c i t) -> p c t i", i=4, t=4), planes.rearrange("p t (c i) -> p c t i", i=4)
-            )
+            engine_copy(as_woven(woven), as_planes(planes))
 
         def quantise(codes, scales, woven, c0, n):
             nc.vector.quantize_mx(out=codes[:, cols(c0, n)].bitcast(FP8X4), scales=scales[:, cols(c0, n)], in_=woven)
@@ -180,134 +187,132 @@ def tile_picked_listsmooth_sigmoid_po_kernel(
         z2_s = new("z2_s", [P, W], U8)
         z_c = new("z_c", [P, W], U32)
         z_s = new("z_s", [P, W], U8)
-        z2_woven = new("z2_woven", [P, 4 * W], BF16)
-        first_half = planes_by_scalar("z2_0", w2_slot, q_words0[:].bitcast(FP8X4), q_scale[:, 0:HALF], HALF, gq_c)
-        third_quarter = planes_by_scalar("z2_2", w2_slot, q_words1[:, 0:P].bitcast(FP8X4), q_scale[:, cols(2 * P, P)], P, gq_c)
-        woven_by_vector(
-            "z2_3", z2_woven[:, cols(4 * 3 * P, 4 * P)], w2_slot, q_words1[:, cols(P, P)].bitcast(FP8X4), q_scale[:, cols(3 * P, P)], gq_c
-        )
-        weave(nc.vector.tensor_copy, z2_woven[:, 0 : 4 * HALF], first_half)
-        weave(nc.vector.tensor_copy, z2_woven[:, cols(4 * 2 * P, 4 * P)], third_quarter)
-        for c0 in (0, HALF):
-            quantise(z2_c, z2_s, z2_woven[:, cols(4 * c0, 4 * HALF)], c0, HALF)
+        z_woven = [new("z_woven%d" % t, [P, 4 * P], BF16) for t in range(4)]
+
+        def q_cols(words, c0, n):
+            return words[:, cols(c0 % HALF, n)].bitcast(FP8X4), q_scale[:, cols(c0, n)]
+
+        def z_by_vector(t):
+            woven_by_vector("z_%d" % t, z_woven[t][:], w1_slot, *k_slot(t), gk_c)
+
+        def quantise_z(t):
+            quantise(z_c, z_s, z_woven[t][:], t * P, P)
+
+        second_quarter = planes_by_scalar("z2_1", w2_slot, *q_cols(q_words0, P, P), P, gq_c)
+        z2_woven0 = new("z2_woven0", [P, 4 * P], BF16)
+        woven_by_vector("z2_0", z2_woven0[:], w2_slot, *q_cols(q_words0, 0, P), gq_c)
+        second_half = planes_by_scalar("z2_2", w2_slot, *q_cols(q_words1, HALF, HALF), HALF, gq_c)
+        quantise(z2_c, z2_s, z2_woven0[:], 0, P)
+        z2_woven1 = new("z2_woven1", [P, 4 * P], BF16, over="w1_raw_s")
+        weave(nc.vector.tensor_copy, z2_woven1[:], second_quarter)
+        z_by_vector(0)
+        quantise(z2_c, z2_s, z2_woven1[:], P, P)
+        z2_woven2 = new("z2_woven2", [P, 4 * HALF], BF16, over="z2_1_planes")
+        weave(nc.vector.tensor_copy, z2_woven2[:], second_half)
+        quantise_z(0)
+        quantise(z2_c, z2_s, z2_woven2[:], HALF, HALF)
 
         wv_woven = new("wv_woven", [P, 4 * W], BF16)
 
-        def weave_wv(engine_copy, h, m0, n):
+        def weave_wv(engine_copy, j):
             engine_copy(
-                wv_woven[:].rearrange("p (t m j) -> p m j t", t=4, j=4)[:, cols(64 * h + m0, n)],
-                wv_raw[h][:].rearrange("p j (m t) -> p m j t", t=4)[:, cols(m0, n)],
+                wv_woven[:].rearrange("p (t m j) -> p m j t", t=4, j=4)[:, wv_cuts[j] // 4 : wv_cuts[j + 1] // 4],
+                wv_raw[j][:].rearrange("p j (m t) -> p m j t", t=4),
             )
 
-        for c0 in (0, HALF):
-            planes = planes_by_scalar(
-                "z_%d" % c0, w1_slot, k_words[:, cols(c0, HALF)].bitcast(FP8X4), k_scale[:, cols(c0, HALF)], HALF, gk_c
+        for j in range(2):
+            weave_wv(nc.scalar.copy, j)
+
+        windows = [new("s_window%d" % t, [P, W], F32, over="wv_raw1" if t == 0 else None) for t in range(4)]
+
+        def scores(t, acc, c0=0, n=W):
+            mx(
+                acc[:, 0:n],
+                z_c[:, cols(t * P, P)].bitcast(FP8X4),
+                z_s[:, cols(t * P, P)],
+                z2_c[:, cols(c0, n)].bitcast(FP8X4),
+                z2_s[:, cols(c0, n)],
             )
-            woven = new("z_woven%d" % c0, [P, 4 * HALF], BF16)
-            if c0 == 0:
-                for j in (0, P):
-                    weave(nc.vector.tensor_copy, woven[:, cols(4 * j, 4 * P)], planes[:, :, cols(j, P)])
-                for j in (0, P):
-                    quantise(z_c, z_s, woven[:, cols(4 * j, 4 * P)], j, P)
+            nc.scalar.activation(windows[t][:, cols(c0, n)], acc[:, 0:n], ACT.Copy, scale=SIXTEENTH)
+
+        sums = [new("sums%d" % h, [P, 4, HALF], F32) for h in range(2)]
+        sig = [new("sig%d" % c, [P, 4, P], F32) for c in range(4)]
+
+        def smooth(t, h, on_vector=False, over=None, adder=nc.gpsimd):
+            fetched = new("fetched%d%d" % (t, h), [P, HALF], F32, over)
+            looked_up = windows[t][:].indirect(entries(nb_sb, h * HALF, HALF))
+            if on_vector:
+                nc.vector.tensor_copy(fetched[:], looked_up)
             else:
-                weave(nc.vector.tensor_copy, woven[:], planes)
-                weave_wv(nc.vector.tensor_copy, 1, 0, 64)
-                quantise(z_c, z_s, woven[:], c0, HALF)
+                nc.scalar.activation(fetched[:], looked_up, ACT.Copy)
+            adder.tensor_tensor(sums[h][:, t, :], windows[t][:, cols(h * HALF, HALF)], fetched[:], ALU.add)
 
-        weave_wv(nc.scalar.copy, 0, 0, 64)
+        def squash(c):
+            nc.scalar.activation(sig[c][:], sums[c // 2][:, :, cols((c % 2) * P, P)], ACT.Sigmoid)
 
-        windows = [new("s_window%d" % t, [P, W], F32) for t in range(4)]
-        plains = {t: new("s_plain%d" % t, [P, W], F32) for t in (2, 3)}
-        for t in range(4):
-            acc = bank("s_acc%d" % t)
-            mx(acc[:], z_c[:, cols(t * P, P)].bitcast(FP8X4), z_s[:, cols(t * P, P)], z2_c[:].bitcast(FP8X4), z2_s[:])
-            nc.scalar.activation(windows[t][:, 0:W], acc[:], ACT.Copy, scale=SIXTEENTH)
-            if t == 2:
-                nc.sync.dma_start(plains[t][:, HALF:], windows[t][:, HALF:])
-            if t == 3:
-                nc.sync.dma_start(plains[t][:], windows[t][:])
-
-        token_cols = turn("g_cols", token_rows, 8)
-        gi_c, gt_c = token_cols[:, 0:4], token_cols[:, 4:8]
+        scores(0, bank("s_acc0"), 0, HALF)
+        first_acc = bank("s_acc1")
+        scores(0, first_acc, HALF, HALF)
+        smooth(0, 0)
+        smooth(0, 1)
+        z_by_vector(1)
+        z_by_vector(2)
+        quantise_z(1)
+        scores(1, first_acc)
+        z_by_vector(3)
+        quantise_z(2)
         wv_c = new("wv_c", [P, W], U32)
         wv_s = new("wv_s", [P, W], U8)
+        weave_wv(nc.vector.tensor_copy, 2)
+        quantise_z(3)
         quantise(wv_c, wv_s, wv_woven[:], 0, W)
-        zv_s = new("zv_s", [P, W], U8)
+        scores(2, bank("s_acc2"))
 
-        sums = new("sums", [P, 4, W], F32)
-        sig = new("sig", [P, 4, W], F32)
-        zp_planes = new("zp_planes", [P, 2, 4, HALF], BF16)
-
-        def smooth(t, c0, n):
-            nc.vector.tensor_tensor(
-                sums[:, t, cols(c0, n)], windows[t][:].indirect(entries(nb_sb, c0, n)), plains[t][:, cols(c0, n)], ALU.add
-            )
-
-        def squash(t, c0, n):
-            nc.scalar.activation(sig[:, t, cols(c0, n)], sums[:, t, cols(c0, n)], ACT.Sigmoid)
-
-        def gate(t, c0, n):
-            nc.scalar.activation(
-                zp_planes[:, c0 // HALF : (c0 + n) // HALF, t, :],
-                sig[:, t, cols(c0, n)].rearrange("p (h c) -> p h c", c=HALF),
-                ACT.Copy,
-                scale=gt_c[:, t : t + 1],
-            )
-
-        first = new("fetched_first", [P, HALF], F32)
-        by_vector = new("fetched_by_vector", [P, 3, HALF], F32)
-        last = new("fetched_last", [P, HALF], F32, over="z_c")
-        pieces = [(0, 0, first[:]), (1, 0, by_vector[:, 0, :]), (0, HALF, by_vector[:, 1, :]), (2, 0, by_vector[:, 2, :]), (1, HALF, last[:])]
-        for n, (t, c0, fetched) in enumerate(pieces):
-            looked_up = windows[t][:].indirect(entries(nb_sb, c0, HALF))
-            if n in (1, 2, 3):
-                nc.vector.tensor_copy(fetched, looked_up)
-            else:
-                nc.scalar.activation(fetched, looked_up, ACT.Copy)
-            nc.gpsimd.tensor_tensor(sums[:, t, cols(c0, HALF)], windows[t][:, cols(c0, HALF)], fetched, ALU.add)
-        squash(1, 0, HALF)
-        squash(0, 0, W)
-        gate(1, 0, HALF)
-        squash(2, 0, HALF)
-        gate(0, 0, W)
-        squash(1, HALF, HALF)
-        gate(2, 0, HALF)
         zv_woven = new("zv_woven", [P, 4 * W], BF16)
+        smooth(1, 0, on_vector=True)
+        smooth(2, 0)
+        scores(3, bank("s_acc3"))
+        smooth(3, 0)
+        smooth(1, 1)
+        smooth(2, 1)
         for c in range(4):
             woven_by_vector(
                 "zv_%d" % c, zv_woven[:, cols(4 * P * c, 4 * P)], k_slot, wv_c[:, cols(c * P, P)].bitcast(FP8X4), wv_s[:, cols(c * P, P)], gi_c
             )
-        smooth(3, 0, HALF)
-        squash(3, 0, HALF)
-        gate(1, HALF, HALF)
-        gate(3, 0, HALF)
-        for step in (smooth, squash, gate):
-            for t in (2, 3):
-                step(t, HALF, HALF)
-
-        zv_c = new("zv_c", [P, W], U32, over="s_plain3")
+        zv_c = new("zv_c", [P, W], U32)
+        zv_s = new("zv_s", [P, W], U8)
         quantise(zv_c, zv_s, zv_woven[:], 0, W)
+        smooth(3, 1, adder=nc.vector)
+        for c in range(4):
+            squash(c)
 
         zp_woven = [new("zp_woven%d" % h, [P, 4 * HALF], BF16) for h in range(2)]
         zp_c = new("zp_c", [P, W], U32)
         zp_s = new("zp_s", [P, W], U8)
-        for h in range(2):
-            for j in (0, P):
-                engine_copy = nc.scalar.copy if (h, j) == (1, 0) else nc.vector.tensor_copy
-                weave(engine_copy, zp_woven[h][:, cols(4 * j, 4 * P)], zp_planes[:, h, :, cols(j, P)])
-            for j in (0, P):
-                quantise(zp_c, zp_s, zp_woven[h][:, cols(4 * j, 4 * P)], h * HALF + j, P)
+
+        def gate(c):
+            nc.vector.tensor_tensor(
+                as_woven(zp_woven[c // 2][:, cols((c % 2) * 4 * P, 4 * P)]),
+                as_planes(sig[c][:]),
+                gt_c.unsqueeze(1).unsqueeze(3).to_broadcast([P, P // 4, 4, 4]),
+                ALU.mult,
+            )
+
+        def quantise_zp(c):
+            quantise(zp_c, zp_s, zp_woven[c // 2][:, cols((c % 2) * 4 * P, 4 * P)], c * P, P)
 
         y_s = new("y_s", [P, W], U8)
+        y_c = new("y_c", [P, W], U32)
         out_rows = out_0.rearrange("(p t) v -> p t v", t=4)
         out_words = out_1[0].rearrange("p n t -> p (n t)").bitcast(I32)
         y_woven = [new("y_woven%d" % h, [P, 4 * HALF], BF16) for h in range(2)]
         y_first = new("y_first", [P, 4, P], F32)
-        y_middle = new("y_middle", [P, 4, HALF], F32, over="zp_woven1")
+        y_middle = new("y_middle", [P, 4, HALF], F32)
         y_last = new("y_last", [P, 4, P], F32)
         ys = (y_first[:], y_middle[:, :, 0:P], y_middle[:, :, P:], y_last[:])
         stores = {0: (y_first, 0, P), 2: (y_middle, P, HALF), 3: (y_last, 3 * P, P)}
-        for c in range(4):
+
+        def result(c):
             quarter = cols(c * P, P)
             acc = bank("out_acc%d" % c)
             for t in range(4):
@@ -326,7 +331,17 @@ def tile_picked_listsmooth_sigmoid_po_kernel(
                 nc.sync.dma_start(out_rows[:, :, cols(c0, n)], y[:])
             weave(nc.vector.tensor_copy if c == 3 else nc.scalar.copy, y_woven[c // 2][:, cols((c % 2) * 4 * P, 4 * P)], ys[c])
 
-        y_c = new("y_c", [P, W], U32)
+        gate(0)
+        gate(1)
+        quantise_zp(0)
+        quantise_zp(1)
+        gate(2)
+        gate(3)
+        quantise_zp(2)
+        quantise_zp(3)
+        for c in range(4):
+            result(c)
+
         quantise(y_c, y_s, y_woven[0][:], 0, HALF)
         for j in (0, P):
             quantise(y_c, y_s, y_woven[1][:, cols(4 * j, 4 * P)], HALF + j, P)

@@ -56,8 +56,8 @@ def tile_picked_listsmooth_sigmoid_po_kernel(
         for raw_s in (w2_raw_s, w1_raw_s):
             nc.vector.memset(raw_s[:].bitcast(I32), 0)
         feature_rows, token_rows = new("feature_rows", [P, P], F32), new("token_rows", [P, P], F32)
-        for rows in (feature_rows, token_rows):
-            nc.vector.memset(rows[:], 0.0)
+        nc.gpsimd.memset(feature_rows[:], 0.0)
+        nc.vector.memset(token_rows[:], 0.0)
         warm_in = new("warm_in", [P, 1], F32)
         nc.vector.memset(warm_in[:], 0.0)
         warm = new("warm", [P, 1], F32)
@@ -72,30 +72,29 @@ def tile_picked_listsmooth_sigmoid_po_kernel(
             nc.sync.dma_start(raw_w[:].bitcast(I32), words[0].bitcast(I32))
             return raw_w
 
-        def load_factor(rows, first_row, g):
-            nc.sync.dma_start(
+        def load_factor(queue, rows, first_row, g):
+            queue.dma_start(
                 rows[first_row : first_row + 4, :].rearrange("t (b r) -> t b r", r=8),
                 g.rearrange("(b t r) o -> t b (r o)", t=4, r=8),
             )
 
+        load_factor(nc.gpsimd, feature_rows, 4, gk)
         nc.sync.dma_start(qs_sb[:], qs)
         w2_raw_w = load_fp4_words("w2_raw_w", w2_words)
         nc.sync.dma_start(offs_sb[:], offs)
         load_scales(xs, x_scales)
         nc.sync.dma_start(xw[:], x_words[0].rearrange("p n t -> p (n t)").bitcast(I32))
-        load_factor(feature_rows, 0, gq)
-        load_factor(feature_rows, 4, gk)
+        load_factor(nc.sync, feature_rows, 0, gq)
         load_scales(w2_raw_s, w2_scales)
         w1_raw_w = load_fp4_words("w1_raw_w", w1_words)
         wv_rows = wv.rearrange("(p j) c -> p j c", j=4)
-        wv_cuts = (0, HALF, 3 * P, W)
-        wv_raw = [new("wv_raw%d" % j, [P, 4, wv_cuts[j + 1] - wv_cuts[j]], F32) for j in range(3)]
+        wv_raw = [new("wv_raw%d" % h, [P, 4, HALF], F32) for h in range(2)]
+        nc.sync.dma_start(wv_raw[0][:], wv_rows[:, :, 0:HALF])
         load_scales(w1_raw_s, w1_scales)
-        for j in range(3):
-            nc.sync.dma_start(wv_raw[j][:], wv_rows[:, :, wv_cuts[j] : wv_cuts[j + 1]])
+        nc.sync.dma_start(wv_raw[1][:], wv_rows[:, :, HALF:])
         nc.sync.dma_start(nb_sb[:], nb)
-        load_factor(token_rows, 0, gi)
-        load_factor(token_rows, 4, gt)
+        load_factor(nc.sync, token_rows, 0, gi)
+        load_factor(nc.sync, token_rows, 4, gt)
         res_sb = new("res_sb", [P, 4, W], F32)
         nc.sync.dma_start(res_sb[:], res.rearrange("(p t) v -> p t v", t=4))
 
@@ -183,6 +182,18 @@ def tile_picked_listsmooth_sigmoid_po_kernel(
                 ALU.mult,
             )
 
+        wv_woven = new("wv_woven", [P, 4 * W], BF16)
+
+        def weave_wv(h):
+            nc.scalar.copy(
+                wv_woven[:].rearrange("p (t m j) -> p m j t", t=4, j=4)[:, cols(64 * h, 64)],
+                wv_raw[h][:].rearrange("p j (m t) -> p m j t", t=4),
+            )
+
+        weave_wv(0)
+        scalar_cols = new("scalar_cols", [P, 8], F32, over="wv_raw0")
+        nc.scalar.copy(scalar_cols[:], features_turned[:, 0:8])
+
         z2_c = new("z2_c", [P, W], U32)
         z2_s = new("z2_s", [P, W], U8)
         z_c = new("z_c", [P, W], U32)
@@ -198,10 +209,10 @@ def tile_picked_listsmooth_sigmoid_po_kernel(
         def quantise_z(t):
             quantise(z_c, z_s, z_woven[t][:], t * P, P)
 
-        second_quarter = planes_by_scalar("z2_1", w2_slot, *q_cols(q_words0, P, P), P, gq_c)
+        second_quarter = planes_by_scalar("z2_1", w2_slot, *q_cols(q_words0, P, P), P, scalar_cols[:, 0:4])
         z2_woven0 = new("z2_woven0", [P, 4 * P], BF16)
         woven_by_vector("z2_0", z2_woven0[:], w2_slot, *q_cols(q_words0, 0, P), gq_c)
-        second_half = planes_by_scalar("z2_2", w2_slot, *q_cols(q_words1, HALF, HALF), HALF, gq_c)
+        second_half = planes_by_scalar("z2_2", w2_slot, *q_cols(q_words1, HALF, HALF), HALF, scalar_cols[:, 0:4])
         quantise(z2_c, z2_s, z2_woven0[:], 0, P)
         z2_woven1 = new("z2_woven1", [P, 4 * P], BF16, over="w1_raw_s")
         weave(nc.vector.tensor_copy, z2_woven1[:], second_quarter)
@@ -212,18 +223,9 @@ def tile_picked_listsmooth_sigmoid_po_kernel(
         quantise_z(0)
         quantise(z2_c, z2_s, z2_woven2[:], HALF, HALF)
 
-        wv_woven = new("wv_woven", [P, 4 * W], BF16)
-
-        def weave_wv(engine_copy, j):
-            engine_copy(
-                wv_woven[:].rearrange("p (t m j) -> p m j t", t=4, j=4)[:, wv_cuts[j] // 4 : wv_cuts[j + 1] // 4],
-                wv_raw[j][:].rearrange("p j (m t) -> p m j t", t=4),
-            )
-
-        for j in range(2):
-            weave_wv(nc.scalar.copy, j)
-
-        windows = [new("s_window%d" % t, [P, W], F32, over="wv_raw1" if t == 0 else None) for t in range(4)]
+        weave_wv(1)
+        z_planes2 = planes_by_scalar("z_2", w1_slot, *k_slot(2), P, scalar_cols[:, 4:8])
+        windows = [new("s_window%d" % t, [P, W], F32) for t in range(4)]
 
         def scores(t, acc, c0=0, n=W):
             mx(
@@ -238,14 +240,22 @@ def tile_picked_listsmooth_sigmoid_po_kernel(
         sums = [new("sums%d" % h, [P, 4, HALF], F32) for h in range(2)]
         sig = [new("sig%d" % c, [P, 4, P], F32) for c in range(4)]
 
-        def smooth(t, h, on_vector=False, over=None, adder=nc.gpsimd):
-            fetched = new("fetched%d%d" % (t, h), [P, HALF], F32, over)
+        fetched = {}
+
+        def fetch(t, h, on_vector=False):
+            fetched[t, h] = new("fetched%d%d" % (t, h), [P, HALF], F32)
             looked_up = windows[t][:].indirect(entries(nb_sb, h * HALF, HALF))
             if on_vector:
-                nc.vector.tensor_copy(fetched[:], looked_up)
+                nc.vector.tensor_copy(fetched[t, h][:], looked_up)
             else:
-                nc.scalar.activation(fetched[:], looked_up, ACT.Copy)
-            adder.tensor_tensor(sums[h][:, t, :], windows[t][:, cols(h * HALF, HALF)], fetched[:], ALU.add)
+                nc.scalar.activation(fetched[t, h][:], looked_up, ACT.Copy)
+
+        def add(t, h, adder=nc.gpsimd):
+            adder.tensor_tensor(sums[h][:, t, :], windows[t][:, cols(h * HALF, HALF)], fetched[t, h][:], ALU.add)
+
+        def smooth(t, h, on_vector=False):
+            fetch(t, h, on_vector)
+            add(t, h)
 
         def squash(c):
             nc.scalar.activation(sig[c][:], sums[c // 2][:, :, cols((c % 2) * P, P)], ACT.Sigmoid)
@@ -256,33 +266,38 @@ def tile_picked_listsmooth_sigmoid_po_kernel(
         smooth(0, 0)
         smooth(0, 1)
         z_by_vector(1)
-        z_by_vector(2)
+        weave(nc.vector.tensor_copy, z_woven[2][:], z_planes2)
         quantise_z(1)
         scores(1, first_acc)
-        z_by_vector(3)
-        quantise_z(2)
         wv_c = new("wv_c", [P, W], U32)
         wv_s = new("wv_s", [P, W], U8)
-        weave_wv(nc.vector.tensor_copy, 2)
-        quantise_z(3)
         quantise(wv_c, wv_s, wv_woven[:], 0, W)
+        quantise_z(2)
+        z_by_vector(3)
+        quantise_z(3)
         scores(2, bank("s_acc2"))
+        scores(3, bank("s_acc3"))
 
         zv_woven = new("zv_woven", [P, 4 * W], BF16)
-        smooth(1, 0, on_vector=True)
-        smooth(2, 0)
-        scores(3, bank("s_acc3"))
-        smooth(3, 0)
-        smooth(1, 1)
-        smooth(2, 1)
-        for c in range(4):
+
+        def zv_by_vector(c):
             woven_by_vector(
                 "zv_%d" % c, zv_woven[:, cols(4 * P * c, 4 * P)], k_slot, wv_c[:, cols(c * P, P)].bitcast(FP8X4), wv_s[:, cols(c * P, P)], gi_c
             )
+
+        zv_by_vector(0)
+        smooth(1, 0, on_vector=True)
+        for t, h in ((2, 0), (3, 0), (1, 1)):
+            smooth(t, h)
+        fetch(2, 1)
+        fetch(3, 1)
+        for c in (1, 2, 3):
+            zv_by_vector(c)
         zv_c = new("zv_c", [P, W], U32)
         zv_s = new("zv_s", [P, W], U8)
         quantise(zv_c, zv_s, zv_woven[:], 0, W)
-        smooth(3, 1, adder=nc.vector)
+        for t in (2, 3):
+            add(t, 1, nc.vector)
         for c in range(4):
             squash(c)
 
@@ -334,12 +349,13 @@ def tile_picked_listsmooth_sigmoid_po_kernel(
         gate(0)
         gate(1)
         quantise_zp(0)
-        quantise_zp(1)
         gate(2)
+        quantise_zp(1)
         gate(3)
         quantise_zp(2)
+        result(0)
         quantise_zp(3)
-        for c in range(4):
+        for c in (1, 2, 3):
             result(c)
 
         quantise(y_c, y_s, y_woven[0][:], 0, HALF)

@@ -56,8 +56,8 @@ def tile_picked_listsmooth_sigmoid_po_kernel(
         for raw_s in (w2_raw_s, w1_raw_s):
             nc.vector.memset(raw_s[:].bitcast(I32), 0)
         feature_rows, token_rows = new("feature_rows", [P, P], F32), new("token_rows", [P, P], F32)
-        nc.gpsimd.memset(feature_rows[:], 0.0)
-        nc.vector.memset(token_rows[:], 0.0)
+        for rows in (feature_rows, token_rows):
+            nc.vector.memset(rows[:], 0.0)
         warm_in = new("warm_in", [P, 1], F32)
         nc.vector.memset(warm_in[:], 0.0)
         warm = new("warm", [P, 1], F32)
@@ -72,29 +72,30 @@ def tile_picked_listsmooth_sigmoid_po_kernel(
             nc.sync.dma_start(raw_w[:].bitcast(I32), words[0].bitcast(I32))
             return raw_w
 
-        def load_factor(queue, rows, first_row, g):
-            queue.dma_start(
+        def load_factor(rows, first_row, g):
+            nc.sync.dma_start(
                 rows[first_row : first_row + 4, :].rearrange("t (b r) -> t b r", r=8),
                 g.rearrange("(b t r) o -> t b (r o)", t=4, r=8),
             )
 
-        load_factor(nc.gpsimd, feature_rows, 4, gk)
         nc.sync.dma_start(qs_sb[:], qs)
         w2_raw_w = load_fp4_words("w2_raw_w", w2_words)
         nc.sync.dma_start(offs_sb[:], offs)
         load_scales(xs, x_scales)
         nc.sync.dma_start(xw[:], x_words[0].rearrange("p n t -> p (n t)").bitcast(I32))
-        load_factor(nc.sync, feature_rows, 0, gq)
+        load_factor(feature_rows, 0, gq)
+        load_factor(feature_rows, 4, gk)
         load_scales(w2_raw_s, w2_scales)
         w1_raw_w = load_fp4_words("w1_raw_w", w1_words)
         wv_rows = wv.rearrange("(p j) c -> p j c", j=4)
-        wv_raw = [new("wv_raw%d" % h, [P, 4, HALF], F32) for h in range(2)]
-        nc.sync.dma_start(wv_raw[0][:], wv_rows[:, :, 0:HALF])
+        wv_cuts = (0, HALF, W)
+        wv_raw = [new("wv_raw%d" % j, [P, 4, wv_cuts[j + 1] - wv_cuts[j]], F32) for j in range(2)]
         load_scales(w1_raw_s, w1_scales)
-        nc.sync.dma_start(wv_raw[1][:], wv_rows[:, :, HALF:])
+        for j in range(2):
+            nc.sync.dma_start(wv_raw[j][:], wv_rows[:, :, wv_cuts[j] : wv_cuts[j + 1]])
         nc.sync.dma_start(nb_sb[:], nb)
-        load_factor(nc.sync, token_rows, 0, gi)
-        load_factor(nc.sync, token_rows, 4, gt)
+        load_factor(token_rows, 0, gi)
+        load_factor(token_rows, 4, gt)
         res_sb = new("res_sb", [P, 4, W], F32)
         nc.sync.dma_start(res_sb[:], res.rearrange("(p t) v -> p t v", t=4))
 
@@ -171,8 +172,7 @@ def tile_picked_listsmooth_sigmoid_po_kernel(
                     nc.scalar.activation(planes[:, t, :], acc[:, cols((t - t0) * n, n)], ACT.Copy, scale=g[:, t : t + 1])
             return planes[:]
 
-        def woven_by_vector(name, woven, lhs_slot, rhs, rhs_s, g):
-            acc = bank(name + "_acc")
+        def woven_by_vector(acc, woven, lhs_slot, rhs, rhs_s, g):
             for t in range(4):
                 mx(acc[:, cols(t * P, P)], *lhs_slot(t), rhs, rhs_s)
             nc.vector.tensor_tensor(
@@ -184,15 +184,11 @@ def tile_picked_listsmooth_sigmoid_po_kernel(
 
         wv_woven = new("wv_woven", [P, 4 * W], BF16)
 
-        def weave_wv(h):
-            nc.scalar.copy(
-                wv_woven[:].rearrange("p (t m j) -> p m j t", t=4, j=4)[:, cols(64 * h, 64)],
-                wv_raw[h][:].rearrange("p j (m t) -> p m j t", t=4),
+        def weave_wv(engine_copy, j):
+            engine_copy(
+                wv_woven[:].rearrange("p (t m j) -> p m j t", t=4, j=4)[:, wv_cuts[j] // 4 : wv_cuts[j + 1] // 4],
+                wv_raw[j][:].rearrange("p j (m t) -> p m j t", t=4),
             )
-
-        weave_wv(0)
-        scalar_cols = new("scalar_cols", [P, 8], F32, over="wv_raw0")
-        nc.scalar.copy(scalar_cols[:], features_turned[:, 0:8])
 
         z2_c = new("z2_c", [P, W], U32)
         z2_s = new("z2_s", [P, W], U8)
@@ -204,15 +200,15 @@ def tile_picked_listsmooth_sigmoid_po_kernel(
             return words[:, cols(c0 % HALF, n)].bitcast(FP8X4), q_scale[:, cols(c0, n)]
 
         def z_by_vector(t):
-            woven_by_vector("z_%d" % t, z_woven[t][:], w1_slot, *k_slot(t), gk_c)
+            woven_by_vector(bank("z_acc%d" % t), z_woven[t][:], w1_slot, *k_slot(t), gk_c)
 
         def quantise_z(t):
             quantise(z_c, z_s, z_woven[t][:], t * P, P)
 
-        second_quarter = planes_by_scalar("z2_1", w2_slot, *q_cols(q_words0, P, P), P, scalar_cols[:, 0:4])
+        second_quarter = planes_by_scalar("z2_1", w2_slot, *q_cols(q_words0, P, P), P, gq_c)
         z2_woven0 = new("z2_woven0", [P, 4 * P], BF16)
-        woven_by_vector("z2_0", z2_woven0[:], w2_slot, *q_cols(q_words0, 0, P), gq_c)
-        second_half = planes_by_scalar("z2_2", w2_slot, *q_cols(q_words1, HALF, HALF), HALF, scalar_cols[:, 0:4])
+        woven_by_vector(bank("z2_acc0"), z2_woven0[:], w2_slot, *q_cols(q_words0, 0, P), gq_c)
+        second_half = planes_by_scalar("z2_2", w2_slot, *q_cols(q_words1, HALF, HALF), HALF, gq_c)
         quantise(z2_c, z2_s, z2_woven0[:], 0, P)
         z2_woven1 = new("z2_woven1", [P, 4 * P], BF16, over="w1_raw_s")
         weave(nc.vector.tensor_copy, z2_woven1[:], second_quarter)
@@ -223,9 +219,9 @@ def tile_picked_listsmooth_sigmoid_po_kernel(
         quantise_z(0)
         quantise(z2_c, z2_s, z2_woven2[:], HALF, HALF)
 
-        weave_wv(1)
-        z_planes2 = planes_by_scalar("z_2", w1_slot, *k_slot(2), P, scalar_cols[:, 4:8])
-        windows = [new("s_window%d" % t, [P, W], F32) for t in range(4)]
+        for j in range(2):
+            weave_wv(nc.scalar.copy, j)
+        windows = [new("s_window%d" % t, [P, W], F32, over="wv_raw1" if t == 0 else None) for t in range(4)]
 
         def scores(t, acc, c0=0, n=W):
             mx(
@@ -266,38 +262,42 @@ def tile_picked_listsmooth_sigmoid_po_kernel(
         smooth(0, 0)
         smooth(0, 1)
         z_by_vector(1)
-        weave(nc.vector.tensor_copy, z_woven[2][:], z_planes2)
+        z_by_vector(2)
         quantise_z(1)
         scores(1, first_acc)
+        z_by_vector(3)
+        quantise_z(2)
         wv_c = new("wv_c", [P, W], U32)
         wv_s = new("wv_s", [P, W], U8)
         quantise(wv_c, wv_s, wv_woven[:], 0, W)
-        quantise_z(2)
-        z_by_vector(3)
         quantise_z(3)
-        scores(2, bank("s_acc2"))
-        scores(3, bank("s_acc3"))
+        zv_acc = [None, first_acc, bank("s_acc2"), bank("s_acc3")]
+        scores(2, zv_acc[2])
+        fetch(1, 1)
+        scores(3, zv_acc[3])
+        zv_acc[0] = bank("zv_acc0")
 
         zv_woven = new("zv_woven", [P, 4 * W], BF16)
 
         def zv_by_vector(c):
             woven_by_vector(
-                "zv_%d" % c, zv_woven[:, cols(4 * P * c, 4 * P)], k_slot, wv_c[:, cols(c * P, P)].bitcast(FP8X4), wv_s[:, cols(c * P, P)], gi_c
+                zv_acc[c], zv_woven[:, cols(4 * P * c, 4 * P)], k_slot, wv_c[:, cols(c * P, P)].bitcast(FP8X4), wv_s[:, cols(c * P, P)], gi_c
             )
 
-        zv_by_vector(0)
         smooth(1, 0, on_vector=True)
-        for t, h in ((2, 0), (3, 0), (1, 1)):
-            smooth(t, h)
-        fetch(2, 1)
+        zv_by_vector(0)
+        add(1, 1)
+        smooth(2, 0)
+        fetch(3, 0)
+        smooth(2, 1)
         fetch(3, 1)
         for c in (1, 2, 3):
             zv_by_vector(c)
         zv_c = new("zv_c", [P, W], U32)
         zv_s = new("zv_s", [P, W], U8)
+        add(3, 0, nc.vector)
         quantise(zv_c, zv_s, zv_woven[:], 0, W)
-        for t in (2, 3):
-            add(t, 1, nc.vector)
+        add(3, 1, nc.vector)
         for c in range(4):
             squash(c)
 

@@ -246,8 +246,13 @@ def tile_picked_listsmooth_sigmoid_po_kernel(
             else:
                 nc.scalar.activation(fetched[t, h][:], looked_up, ACT.Copy)
 
-        def add(t, h, adder=nc.gpsimd):
-            adder.tensor_tensor(sums[h][:, t, :], windows[t][:, cols(h * HALF, HALF)], fetched[t, h][:], ALU.add)
+        def add(t, h):
+            nc.gpsimd.tensor_tensor(sums[h][:, t, :], windows[t][:, cols(h * HALF, HALF)], fetched[t, h][:], ALU.add)
+
+        def add_out_of_bank(acc, t, h):
+            nc.vector.scalar_tensor_tensor(
+                sums[h][:, t, :], acc[:, cols(h * HALF, HALF)], SIXTEENTH, fetched[t, h][:], ALU.mult, ALU.add
+            )
 
         def smooth(t, h, on_vector=False):
             fetch(t, h, on_vector)
@@ -271,11 +276,13 @@ def tile_picked_listsmooth_sigmoid_po_kernel(
         wv_s = new("wv_s", [P, W], U8)
         quantise(wv_c, wv_s, wv_woven[:], 0, W)
         quantise_z(3)
-        zv_acc = [None, first_acc, bank("s_acc2"), bank("s_acc3")]
+        zv_acc = [None, first_acc, bank("s_acc2"), None]
+        last_acc = bank("s_acc3")
         scores(2, zv_acc[2])
         fetch(1, 1)
-        scores(3, zv_acc[3])
-        zv_acc[0] = bank("zv_acc0")
+        scores(3, last_acc)
+        for c in (0, 3):
+            zv_acc[c] = bank("zv_acc%d" % c)
 
         zv_woven = new("zv_woven", [P, 4 * W], BF16)
 
@@ -295,9 +302,9 @@ def tile_picked_listsmooth_sigmoid_po_kernel(
             zv_by_vector(c)
         zv_c = new("zv_c", [P, W], U32)
         zv_s = new("zv_s", [P, W], U8)
-        add(3, 0, nc.vector)
+        add_out_of_bank(last_acc, 3, 0)
         quantise(zv_c, zv_s, zv_woven[:], 0, W)
-        add(3, 1, nc.vector)
+        add_out_of_bank(last_acc, 3, 1)
         for c in range(4):
             squash(c)
 

@@ -126,12 +126,13 @@ def tile_picked_listsmooth_sigmoid_po_kernel(
         nc.vector.tensor_copy(q_scale[:], xs[:].indirect(qs_sb[:]))
         k_scale = new("k_scale", [P, W], U8)
         nc.vector.tensor_copy(dealt_by_slot(k_scale), xs[:].indirect(offs_sb[:]))
-        q_words0 = new("q_words0", [P, HALF], U32)
-        nc.vector.tensor_copy(q_words0[:], xw[:].bitcast(U32).indirect(entries(qs_sb, 0, HALF)))
+        q_cuts = (0, P, HALF, W)
+        q_words = [new("q_words%d" % j, [P, q_cuts[j + 1] - q_cuts[j]], U32) for j in range(3)]
+        for j in range(3):
+            picked = entries(qs_sb, q_cuts[j], q_cuts[j + 1] - q_cuts[j])
+            nc.vector.tensor_copy(q_words[j][:], xw[:].bitcast(U32).indirect(picked))
         w2_w = deal("w2_w", w2_raw_w, 2 * W)
         w2_s = deal("w2_s", w2_raw_s, W)
-        q_words1 = new("q_words1", [P, HALF], U32)
-        nc.vector.tensor_copy(q_words1[:], xw[:].bitcast(U32).indirect(entries(qs_sb, HALF, HALF)))
         k_words = new("k_words", [P, W], U32)
         nc.vector.tensor_copy(dealt_by_slot(k_words), xw[:].bitcast(U32).indirect(offs_sb[:]))
         w1_w = deal("w1_w", w1_raw_w, 2 * W)
@@ -196,8 +197,8 @@ def tile_picked_listsmooth_sigmoid_po_kernel(
         z_s = new("z_s", [P, W], U8)
         z_woven = [new("z_woven%d" % t, [P, 4 * P], BF16) for t in range(4)]
 
-        def q_cols(words, c0, n):
-            return words[:, cols(c0 % HALF, n)].bitcast(FP8X4), q_scale[:, cols(c0, n)]
+        def q_piece(j):
+            return q_words[j][:].bitcast(FP8X4), q_scale[:, q_cuts[j] : q_cuts[j + 1]]
 
         def z_by_vector(t):
             woven_by_vector(bank("z_acc%d" % t), z_woven[t][:], w1_slot, *k_slot(t), gk_c)
@@ -205,15 +206,15 @@ def tile_picked_listsmooth_sigmoid_po_kernel(
         def quantise_z(t):
             quantise(z_c, z_s, z_woven[t][:], t * P, P)
 
-        second_quarter = planes_by_scalar("z2_1", w2_slot, *q_cols(q_words0, P, P), P, gq_c)
+        second_quarter = planes_by_scalar("z2_1", w2_slot, *q_piece(0), P, gq_c)
         z2_woven0 = new("z2_woven0", [P, 4 * P], BF16)
-        woven_by_vector(bank("z2_acc0"), z2_woven0[:], w2_slot, *q_cols(q_words0, 0, P), gq_c)
-        second_half = planes_by_scalar("z2_2", w2_slot, *q_cols(q_words1, HALF, HALF), HALF, gq_c)
-        quantise(z2_c, z2_s, z2_woven0[:], 0, P)
+        woven_by_vector(bank("z2_acc0"), z2_woven0[:], w2_slot, *q_piece(1), gq_c)
+        second_half = planes_by_scalar("z2_2", w2_slot, *q_piece(2), HALF, gq_c)
+        quantise(z2_c, z2_s, z2_woven0[:], P, P)
         z2_woven1 = new("z2_woven1", [P, 4 * P], BF16, over="w1_raw_s")
         weave(nc.vector.tensor_copy, z2_woven1[:], second_quarter)
         z_by_vector(0)
-        quantise(z2_c, z2_s, z2_woven1[:], P, P)
+        quantise(z2_c, z2_s, z2_woven1[:], 0, P)
         z2_woven2 = new("z2_woven2", [P, 4 * HALF], BF16, over="z2_1_planes")
         weave(nc.vector.tensor_copy, z2_woven2[:], second_half)
         quantise_z(0)

from contextlib import ExitStack

import concourse.mybir as mybir
from concourse.masks import make_identity

FLOPS = 5 * 2 * 512 * 512 * 512

F32 = mybir.dt.float32
BF16 = mybir.dt.bfloat16
I32 = mybir.dt.int32
U32 = mybir.dt.uint32
U16 = mybir.dt.uint16
U8 = mybir.dt.uint8
FP8X4 = mybir.dt.float8_e4m3fn_x4
FP4X4 = mybir.dt.float4_e2m1fn_x4
ACT = mybir.ActivationFunctionType
ALU = mybir.AluOpType

P = 128
T = 2048
W = 512
HALF = W // 2
ENTRIES = 16
SIXTEENTH = 0.0625


def tile_picked_listsmooth_sigmoid_po_kernel(
    tc, x_words, x_scales, w1_words, w1_scales, w2_words, w2_scales, gk, gq, wv, gi, res, gt, offs, qs, nb, out_0, out_1, out_2
):
    nc = tc.nc
    with ExitStack() as ctx:
        lists = ctx.enter_context(tc.tile_pool(name="lists", bufs=1))
        sb = ctx.enter_context(tc.tile_pool(name="sb", bufs=1))
        psum = ctx.enter_context(tc.psum_pool(name="psum", bufs=7))
        held = ctx.enter_context(tc.psum_pool(name="held", bufs=1))

        def new(name, shape, dtype, over=None):
            return sb.tile(shape, dtype, name=name, tag=over or name, align_bytes=64)

        def bank(name):
            return psum.tile([P, W], F32, name=name, tag="bank")

        def cols(c0, n):
            return slice(c0, c0 + n)

        def entries(offsets, c0, n):
            return offsets[:, c0 // ENTRIES : (c0 + n) // ENTRIES]

        qs_sb = lists.tile([P, W // ENTRIES], U16, name="qs_sb")
        offs_sb = lists.tile([P, W // ENTRIES], U16, name="offs_sb")
        nb_sb = lists.tile([P, W // ENTRIES], U16, name="nb_sb")
        xs = new("xs", [P, T], U8)
        xw = new("xw", [P, T], I32)
        nc.vector.memset(xs[:].bitcast(I32), 0)
        w2_raw_s, w1_raw_s = new("w2_raw_s", [P, W], U8), new("w1_raw_s", [P, W], U8)
        for raw_s in (w2_raw_s, w1_raw_s):
            nc.vector.memset(raw_s[:].bitcast(I32), 0)
        feature_rows, token_rows = new("feature_rows", [P, P], F32), new("token_rows", [P, P], F32)
        for rows in (feature_rows, token_rows):
            nc.vector.memset(rows[:], 0.0)
        warm_in = new("warm_in", [P, 1], F32)
        nc.vector.memset(warm_in[:], 0.0)
        warm = new("warm", [P, 1], F32)
        nc.scalar.activation(warm[:], warm_in[:], ACT.Sigmoid)

        def load_scales(tile, scales):
            for r in range(4):
                nc.sync.dma_start(tile[r:P:32, :].bitcast(I32), scales[0, r:16:4, :].bitcast(I32))

        def load_fp4_words(name, words):
            raw_w = new(name, [P, 2 * W], U8)
            nc.sync.dma_start(raw_w[:].bitcast(I32), words[0].bitcast(I32))
            return raw_w

        def load_factor(rows, first_row, g):
            nc.sync.dma_start(
                rows[first_row : first_row + 4, :].rearrange("t (b r) -> t b r", r=8),
                g.rearrange("(b t r) o -> t b (r o)", t=4, r=8),
            )

        nc.sync.dma_start(qs_sb[:], qs)
        w2_raw_w = load_fp4_words("w2_raw_w", w2_words)
        nc.sync.dma_start(offs_sb[:], offs)
        load_scales(xs, x_scales)
        nc.sync.dma_start(xw[:], x_words[0].rearrange("p n t -> p (n t)").bitcast(I32))
        load_factor(feature_rows, 0, gq)
        load_factor(feature_rows, 4, gk)
        load_scales(w2_raw_s, w2_scales)
        w1_raw_w = load_fp4_words("w1_raw_w", w1_words)
        wv_rows = wv.rearrange("(p j) c -> p j c", j=4)
        wv_cuts = (0, HALF, W)
        wv_raw = [new("wv_raw%d" % j, [P, 4, wv_cuts[j + 1] - wv_cuts[j]], F32) for j in range(2)]
        load_scales(w1_raw_s, w1_scales)
        for j in range(2):
            nc.sync.dma_start(wv_raw[j][:], wv_rows[:, :, wv_cuts[j] : wv_cuts[j + 1]])
        nc.sync.dma_start(nb_sb[:], nb)
        load_factor(token_rows, 0, gi)
        load_factor(token_rows, 4, gt)
        res_sb = new("res_sb", [P, 4, W], F32)
        nc.sync.dma_start(res_sb[:], res.rearrange("(p t) v -> p t v", t=4))

        ident = new("ident", [P, P], F32)
        make_identity(nc, ident[:])
        features_turned = bank("features_turned")
        nc.tensor.transpose(features_turned[:, 0:P], feature_rows[:], ident[:])
        feature_cols = new("feature_cols", [P, 8], F32)
        nc.scalar.copy(feature_cols[:], features_turned[:, 0:8])
        tokens_turned = held.tile([P, P], F32, name="tokens_turned")
        nc.tensor.transpose(tokens_turned[:], token_rows[:], ident[:])
        gi_cols = new("gi_cols", [P, 4], F32)
        nc.scalar.copy(gi_cols[:], tokens_turned[:, 0:4])
        gq_c, gk_c, gi_c, gt_c = feature_cols[:, 0:4], feature_cols[:, 4:8], gi_cols[:], tokens_turned[:, 4:8]

        def deal(name, raw, width):
            dealt = new(name, [P, width], U8)
            nc.gpsimd.tensor_copy(
                dealt[:].bitcast(I32).rearrange("p (t b u) -> p t b u", t=4, b=16),
                raw[:].bitcast(I32).rearrange("p (b t u) -> p t b u", t=4, b=16),
            )
            return dealt

        def dealt_by_slot(tile):
            return tile[:].rearrange("p (t b r) -> p b t r", t=4, b=16)

        q_scale = new("q_scale", [P, W], U8)
        nc.vector.tensor_copy(q_scale[:], xs[:].indirect(qs_sb[:]))
        k_scale = new("k_scale", [P, W], U8)
        nc.vector.tensor_copy(dealt_by_slot(k_scale), xs[:].indirect(offs_sb[:]))
        q_cuts = (0, P, HALF, W)
        q_words = [new("q_words%d" % j, [P, q_cuts[j + 1] - q_cuts[j]], U32) for j in range(3)]
        for j in range(3):
            picked = entries(qs_sb, q_cuts[j], q_cuts[j + 1] - q_cuts[j])
            nc.vector.tensor_copy(q_words[j][:], xw[:].bitcast(U32).indirect(picked))
        w2_w = deal("w2_w", w2_raw_w, 2 * W)
        w2_s = deal("w2_s", w2_raw_s, W)
        k_words = new("k_words", [P, W], U32)
        nc.vector.tensor_copy(dealt_by_slot(k_words), xw[:].bitcast(U32).indirect(offs_sb[:]))
        w1_w = deal("w1_w", w1_raw_w, 2 * W)
        w1_s = deal("w1_s", w1_raw_s, W)

        def mx(out, lhs, lhs_s, rhs, rhs_s):
            nc.tensor.matmul_mx(out=out, lhsT=lhs, lhsT_scale=lhs_s, rhs=rhs, rhs_scale=rhs_s, start=True, stop=True)

        def w2_slot(t):
            return w2_w[:, cols(2 * P * t, 2 * P)].bitcast(FP4X4), w2_s[:, cols(t * P, P)]

        def w1_slot(t):
            return w1_w[:, cols(2 * P * t, 2 * P)].bitcast(FP4X4), w1_s[:, cols(t * P, P)]

        def k_slot(t):
            return k_words[:, cols(t * P, P)].bitcast(FP8X4), k_scale[:, cols(t * P, P)]

        def as_woven(woven):
            return woven.rearrange("p (c i t) -> p c t i", i=4, t=4)

        def as_planes(planes):
            return planes.rearrange("p t (c i) -> p c t i", i=4)

        def weave(engine_copy, woven, planes):
            engine_copy(as_woven(woven), as_planes(planes))

        def quantise(codes, scales, woven, c0, n):
            nc.vector.quantize_mx(out=codes[:, cols(c0, n)].bitcast(FP8X4), scales=scales[:, cols(c0, n)], in_=woven)

        def planes_by_scalar(name, lhs_slot, rhs, rhs_s, n, g):
            planes = new(name + "_planes", [P, 4, n], BF16)
            per_bank = W // n
            for t0 in range(0, 4, per_bank):
                acc = bank(name + "_acc%d" % t0)
                for t in range(t0, t0 + per_bank):
                    mx(acc[:, cols((t - t0) * n, n)], *lhs_slot(t), rhs, rhs_s)
                for t in range(t0, t0 + per_bank):
                    nc.scalar.activation(planes[:, t, :], acc[:, cols((t - t0) * n, n)], ACT.Copy, scale=g[:, t : t + 1])
            return planes[:]

        def woven_by_vector(acc, woven, lhs_slot, rhs, rhs_s, g):
            for t in range(4):
                mx(acc[:, cols(t * P, P)], *lhs_slot(t), rhs, rhs_s)
            nc.vector.tensor_tensor(
                woven.rearrange("p (n t) -> p n t", t=4),
                acc[:].rearrange("p (t n) -> p n t", t=4),
                g.unsqueeze(1).to_broadcast([P, P, 4]),
                ALU.mult,
            )

        wv_woven = new("wv_woven", [P, 4 * W], BF16)

        def weave_wv(engine_copy, j):
            engine_copy(
                wv_woven[:].rearrange("p (t m j) -> p m j t", t=4, j=4)[:, wv_cuts[j] // 4 : wv_cuts[j + 1] // 4],
                wv_raw[j][:].rearrange("p j (m t) -> p m j t", t=4),
            )

        z2_c = new("z2_c", [P, W], U32)
        z2_s = new("z2_s", [P, W], U8)
        z_c = new("z_c", [P, W], U32)
        z_s = new("z_s", [P, W], U8)
        z_woven = [new("z_woven%d" % t, [P, 4 * P], BF16) for t in range(4)]

        def q_piece(j):
            return q_words[j][:].bitcast(FP8X4), q_scale[:, q_cuts[j] : q_cuts[j + 1]]

        def z_by_vector(t):
            woven_by_vector(bank("z_acc%d" % t), z_woven[t][:], w1_slot, *k_slot(t), gk_c)

        def quantise_z(t):
            quantise(z_c, z_s, z_woven[t][:], t * P, P)

        second_quarter = planes_by_scalar("z2_1", w2_slot, *q_piece(0), P, gq_c)
        z2_woven0 = new("z2_woven0", [P, 4 * P], BF16)
        woven_by_vector(bank("z2_acc0"), z2_woven0[:], w2_slot, *q_piece(1), gq_c)
        second_half = planes_by_scalar("z2_2", w2_slot, *q_piece(2), HALF, gq_c)
        quantise(z2_c, z2_s, z2_woven0[:], P, P)
        z2_woven1 = new("z2_woven1", [P, 4 * P], BF16, over="w1_raw_s")
        weave(nc.vector.tensor_copy, z2_woven1[:], second_quarter)
        z_by_vector(0)
        quantise(z2_c, z2_s, z2_woven1[:], 0, P)
        z2_woven2 = new("z2_woven2", [P, 4 * HALF], BF16, over="z2_1_planes")
        weave(nc.vector.tensor_copy, z2_woven2[:], second_half)
        quantise_z(0)
        quantise(z2_c, z2_s, z2_woven2[:], HALF, HALF)

        for j in range(2):
            weave_wv(nc.scalar.copy, j)
        windows = [new("s_window%d" % t, [P, W], F32, over="wv_raw1" if t == 0 else None) for t in range(4)]

        def scores(t, acc, c0=0, n=W):
            mx(
                acc[:, 0:n],
                z_c[:, cols(t * P, P)].bitcast(FP8X4),
                z_s[:, cols(t * P, P)],
                z2_c[:, cols(c0, n)].bitcast(FP8X4),
                z2_s[:, cols(c0, n)],
            )
            nc.scalar.activation(windows[t][:, cols(c0, n)], acc[:, 0:n], ACT.Copy, scale=SIXTEENTH)

        sums = [new("sums%d" % h, [P, 4, HALF], F32) for h in range(2)]
        sig = [new("sig%d" % c, [P, 4, P], F32) for c in range(4)]

        fetched = {}

        def fetch(t, h, on_vector=False):
            fetched[t, h] = new("fetched%d%d" % (t, h), [P, HALF], F32)
            looked_up = windows[t][:].indirect(entries(nb_sb, h * HALF, HALF))
            if on_vector:
                nc.vector.tensor_copy(fetched[t, h][:], looked_up)
            else:
                nc.scalar.activation(fetched[t, h][:], looked_up, ACT.Copy)

        def add(t, h):
            nc.gpsimd.tensor_tensor(sums[h][:, t, :], windows[t][:, cols(h * HALF, HALF)], fetched[t, h][:], ALU.add)

        def add_out_of_bank(acc, t, h):
            nc.vector.scalar_tensor_tensor(
                sums[h][:, t, :], acc[:, cols(h * HALF, HALF)], SIXTEENTH, fetched[t, h][:], ALU.mult, ALU.add
            )

        def smooth(t, h, on_vector=False):
            fetch(t, h, on_vector)
            add(t, h)

        def squash(c):
            nc.scalar.activation(sig[c][:], sums[c // 2][:, :, cols((c % 2) * P, P)], ACT.Sigmoid)

        scores(0, bank("s_acc0"), 0, HALF)
        first_acc = bank("s_acc1")
        scores(0, first_acc, HALF, HALF)
        smooth(0, 0)
        smooth(0, 1)
        z_by_vector(1)
        z_by_vector(2)
        quantise_z(1)
        scores(1, first_acc)
        z_by_vector(3)
        quantise_z(2)
        wv_c = new("wv_c", [P, W], U32)
        wv_s = new("wv_s", [P, W], U8)
        quantise(wv_c, wv_s, wv_woven[:], 0, W)
        quantise_z(3)
        zv_acc = [None, first_acc, bank("s_acc2"), None]
        last_acc = bank("s_acc3")
        scores(2, zv_acc[2])
        fetch(1, 1)
        scores(3, last_acc)
        for c in (0, 3):
            zv_acc[c] = bank("zv_acc%d" % c)

        zv_woven = new("zv_woven", [P, 4 * W], BF16)

        def zv_by_vector(c):
            woven_by_vector(
                zv_acc[c], zv_woven[:, cols(4 * P * c, 4 * P)], k_slot, wv_c[:, cols(c * P, P)].bitcast(FP8X4), wv_s[:, cols(c * P, P)], gi_c
            )

        smooth(1, 0, on_vector=True)
        zv_by_vector(0)
        add(1, 1)
        smooth(2, 0)
        fetch(3, 0)
        smooth(2, 1)
        fetch(3, 1)
        for c in (1, 2, 3):
            zv_by_vector(c)
        zv_c = new("zv_c", [P, W], U32)
        zv_s = new("zv_s", [P, W], U8)
        add_out_of_bank(last_acc, 3, 0)
        quantise(zv_c, zv_s, zv_woven[:], 0, W)
        add_out_of_bank(last_acc, 3, 1)
        for c in range(4):
            squash(c)

        zp_woven = [new("zp_woven%d" % h, [P, 4 * HALF], BF16) for h in range(2)]
        zp_c = new("zp_c", [P, W], U32)
        zp_s = new("zp_s", [P, W], U8)

        def gate(c):
            nc.vector.tensor_tensor(
                as_woven(zp_woven[c // 2][:, cols((c % 2) * 4 * P, 4 * P)]),
                as_planes(sig[c][:]),
                gt_c.unsqueeze(1).unsqueeze(3).to_broadcast([P, P // 4, 4, 4]),
                ALU.mult,
            )

        def quantise_zp(c):
            quantise(zp_c, zp_s, zp_woven[c // 2][:, cols((c % 2) * 4 * P, 4 * P)], c * P, P)

        y_s = new("y_s", [P, W], U8)
        y_c = new("y_c", [P, W], U32)
        out_rows = out_0.rearrange("(p t) v -> p t v", t=4)
        out_words = out_1[0].rearrange("p n t -> p (n t)").bitcast(I32)
        y_woven = [new("y_woven%d" % h, [P, 4 * HALF], BF16) for h in range(2)]
        y_first = new("y_first", [P, 4, P], F32)
        y_middle = new("y_middle", [P, 4, HALF], F32)
        y_last = new("y_last", [P, 4, P], F32)
        ys = (y_first[:], y_middle[:, :, 0:P], y_middle[:, :, P:], y_last[:])
        stores = {0: (y_first, 0, P), 2: (y_middle, P, HALF), 3: (y_last, 3 * P, P)}

        def result(c):
            quarter = cols(c * P, P)
            acc = bank("out_acc%d" % c)
            for t in range(4):
                mx(
                    acc[:, cols(t * P, P)],
                    zv_c[:, cols(t * P, P)].bitcast(FP8X4),
                    zv_s[:, cols(t * P, P)],
                    zp_c[:, quarter].bitcast(FP8X4),
                    zp_s[:, quarter],
                )
            nc.vector.scalar_tensor_tensor(
                ys[c], acc[:].rearrange("p (t n) -> p t n", t=4), SIXTEENTH, res_sb[:, :, quarter], ALU.mult, ALU.add
            )
            if c in stores:
                y, c0, n = stores[c]
                nc.sync.dma_start(out_rows[:, :, cols(c0, n)], y[:])
            weave(nc.vector.tensor_copy if c == 3 else nc.scalar.copy, y_woven[c // 2][:, cols((c % 2) * 4 * P, 4 * P)], ys[c])

        gate(0)
        gate(1)
        quantise_zp(0)
        gate(2)
        quantise_zp(1)
        gate(3)
        quantise_zp(2)
        result(0)
        quantise_zp(3)
        for c in (1, 2, 3):
            result(c)

        quantise(y_c, y_s, y_woven[0][:], 0, HALF)
        for j in (0, P):
            quantise(y_c, y_s, y_woven[1][:, cols(4 * j, 4 * P)], HALF + j, P)
        nc.sync.dma_start(out_words, y_c[:].bitcast(I32))
        for r in range(4):
            (nc.scalar if r % 2 else nc.sync).dma_start(out_2[0, r:16:4, :].bitcast(I32), y_s[r:P:32, :].bitcast(I32))
